import numpy as np
import ml_dtypes


def mxq(x, axis, fmt="e4m3"):
    dtype, down = {"e4m3": (ml_dtypes.float8_e4m3fn, 7), "e5m2": (ml_dtypes.float8_e5m2, 14)}[fmt]
    v = np.moveaxis(np.asarray(x, np.float32).astype(ml_dtypes.bfloat16).astype(np.float64), axis, -1)
    blocks = v.reshape(v.shape[:-1] + (-1, 32))
    amax = np.abs(blocks).max(-1, keepdims=True)
    byte = np.maximum(np.where(amax > 0, np.frexp(amax)[1] - 1 + 127, 0) - down, 1)
    scale = np.exp2(byte - 127.0)
    codes = (blocks / scale).astype(np.float32).astype(dtype).astype(np.float64)
    return np.moveaxis((codes * scale).reshape(v.shape), -1, axis)


WIDE = False


def mx_kscale(k):
    if not WIDE:
        return np.ones(k)
    levels = np.array([10, -10, 5, -5, 0])
    if k % 512:
        return np.exp2(np.random.permutation(np.resize(levels, k // 32))).repeat(32)
    a = np.empty((k // 512, 16))
    for p in range(k // 512):
        a[p, :8] = np.random.permutation(np.resize(levels, 8))
        for g in range(8):
            far = levels[np.abs(levels - a[p, g]) >= 10]
            a[p, g + 8] = far[np.random.randint(len(far))]
    return np.exp2(a.ravel()).repeat(32)


BF16 = ml_dtypes.bfloat16


def bf(x):
    return np.asarray(x, np.float32).astype(BF16)


def f64(x):
    return np.asarray(x).astype(np.float64)


E2M1 = np.array([0.0, 0.5, 1.0, 1.5, 2.0, 3.0, 4.0, 6.0, -0.0, -0.5, -1.0, -1.5, -2.0, -3.0, -4.0, -6.0])


def pack_weight(w, fmt):
    k, n = w.shape
    w = f64(bf(w)).reshape(k // 32, 32, n)
    amax = np.abs(w).max(1)
    if fmt == "e4m3":
        byte = np.frexp(amax)[1] - 1 + 127 - 7
    else:
        mant, ex = np.frexp(amax / 6.0)
        byte = np.where(mant > 0.5, ex, ex - 1) + 127
    byte = np.clip(np.where(amax > 0, byte, 1), 1, 254)
    scaled = (w * np.exp2(127.0 - byte)[:, None, :]).reshape(k, n).astype(np.float32)
    by_word = np.ascontiguousarray(scaled.reshape(k // 512, 128, 4, n).transpose(0, 1, 3, 2))
    if fmt == "e4m3":
        words = by_word.astype(ml_dtypes.float8_e4m3fn).view(np.uint8)
    else:
        c = by_word.astype(ml_dtypes.float4_e2m1fn).view(np.uint8) & 0xF
        words = c[..., 0::2] | (c[..., 1::2] << 4)
    return np.ascontiguousarray(words), np.ascontiguousarray(byte.astype(np.uint8).reshape(k // 512, 16, n))


def unpack_weight(words, scales, fmt):
    g, p, n, _ = words.shape
    if fmt == "e4m3":
        vals = np.ascontiguousarray(words).view(ml_dtypes.float8_e4m3fn).astype(np.float64)
    else:
        nib = np.empty((g, p, n, 4), np.uint8)
        nib[..., 0::2] = words & 0xF
        nib[..., 1::2] = words >> 4
        vals = E2M1[nib]
    vals = vals * np.repeat(np.exp2(scales.astype(np.float64) - 127.0), 8, axis=1)[..., None]
    return vals.transpose(0, 1, 3, 2).reshape(g * 512, n)
def pack4(w):
    words, scales = pack_weight(w, "e2m1")
    return words.reshape(words.shape[0], 128, -1), scales


def unpack4(words, scales):
    return unpack_weight(words.reshape(words.shape[0], 128, -1, 2), scales, "e2m1")


def planes(Y):
    n, m = Y.shape
    b = f64(bf(Y)).reshape(n // 32, 32, m)
    amax = np.abs(b).max(1)
    byte = np.clip(np.where(amax > 0, np.frexp(amax)[1] - 1 + 127 - 7, 1), 1, 254)
    codes = (b * np.exp2(127.0 - byte)[:, None, :]).reshape(n, m).astype(np.float32).astype(ml_dtypes.float8_e4m3fn).view(np.uint8)
    words = codes.reshape(n // 512, 128, 4, m).transpose(0, 1, 3, 2)
    return np.ascontiguousarray(words), np.ascontiguousarray(byte.astype(np.uint8).reshape(n // 512, 16, m))


S, T, V, B, P = 1024, 2048, 512, 1024, 1536

def setup_inputs():
    rn = np.random.randn
    s, v, t = mx_kscale(T), mx_kscale(V), mx_kscale(B)
    ref_dev = bf(rn(S, T) * s)
    placed_dev = bf(rn(S, V) * v)
    ref_words, ref_scales = pack4(rn(T, B) / np.sqrt(2 * T) / s[:, None])
    placed_inc = bf(rn(V, B) / np.sqrt(2 * V) / v[:, None])
    root_length = bf(np.exp(0.3 * rn(B)) * t)
    panel_words, panel_scales = pack_weight(rn(B, P) / np.sqrt(B) / t[:, None], "e4m3")
    sample_weight = bf(np.exp(0.2 * rn(S)))
    offset = bf(0.4 * rn(P))
    panel_weight = bf(np.exp(0.8 * rn(P)))
    return dict(ref_dev=ref_dev, placed_dev=placed_dev, ref_words=ref_words, ref_scales=ref_scales,
                placed_inc=placed_inc, root_length=root_length, panel_words=panel_words,
                panel_scales=panel_scales, sample_weight=sample_weight, offset=offset,
                panel_weight=panel_weight)

def reference(ref_dev, placed_dev, ref_words, ref_scales, placed_inc, root_length,
              panel_words, panel_scales, sample_weight, offset, panel_weight):
    from_ref = mxq(f64(ref_dev), 1, "e4m3") @ unpack4(ref_words, ref_scales)
    from_placed = mxq(f64(placed_dev), 1, "e4m3") @ mxq(f64(placed_inc), 0, "e4m3")
    E = (from_ref + from_placed) * f64(root_length)
    G = mxq(E, 1, "e4m3") @ unpack_weight(panel_words, panel_scales, "e4m3")
    y = (G * f64(sample_weight)[:, None] + f64(offset)) * f64(panel_weight)
    Y = y.T
    words, scales = planes(Y)
    return y, words, scales

@@ -1,0 +1,382 @@
+from contextlib import ExitStack
+
+import concourse.mybir as mybir
+from concourse.masks import make_identity
+
+S, T, V, B, P = 1024, 2048, 512, 1024, 1536
+FLOPS = 2 * S * (T + V) * B + 2 * S * B * P
+
+F32 = mybir.dt.float32
+BF16 = mybir.dt.bfloat16
+I32 = mybir.dt.int32
+U32 = mybir.dt.uint32
+U8 = mybir.dt.uint8
+FP8X4 = mybir.dt.float8_e4m3fn_x4
+FP4X4 = mybir.dt.float4_e2m1fn_x4
+MULT = mybir.AluOpType.mult
+ADD = mybir.AluOpType.add
+
+NP = 128
+BANK = 512
+TILES = S // NP
+REF_PASSES = T // 512
+E_PASSES = B // 512
+Y_GROUPS = P // 512
+STORE_RUNS = [(0, 1), (1, 3), (3, 5), (5, 7), (7, 8)]
+
+
+def tile_community_branch_gram_k6_kernel(
+    tc, ref_dev, placed_dev, ref_words, ref_scales, placed_inc, root_length,
+    panel_words, panel_scales, sample_weight, offset, panel_weight, out_0, out_1, out_2,
+):
+    nc = tc.nc
+    with ExitStack() as ctx:
+        sb = ctx.enter_context(tc.tile_pool(name="sb", bufs=1))
+        ps = ctx.enter_context(tc.psum_pool(name="ps", bufs=1))
+        ctx.enter_context(tc.manual_schedule())
+
+        def tiles(name, count, shape, dtype):
+            return [sb.tile(shape, dtype, name="%s%d" % (name, i), align_bytes=64) for i in range(count)]
+
+        banks = [ps.tile([NP, BANK], F32, name="bank%d" % i) for i in range(8)]
+        taken = []
+
+        def take_bank():
+            taken.append(0)
+            return banks[(len(taken) - 1) % len(banks)]
+
+        ident = tiles("ident", 1, [NP, NP], F32)[0]
+        rows = tiles("rows", 1, [NP, NP], F32)[0]
+        sw_rows = tiles("sw_rows", 1, [32, NP], BF16)[0]
+        cols = tiles("cols", 1, [NP, 64], F32)[0]
+        root = tiles("root", 1, [NP, B // 2], F32)[0]
+        panel = tiles("panel", 1, [NP, P], F32)[0]
+        ref = tiles("ref", TILES, [NP, T // 2], F32)
+        placed = tiles("placed", TILES // 2, [NP, 2, V // 2], F32)
+        w_codes = tiles("w_codes", E_PASSES, [NP, REF_PASSES, 2 * BANK], U8)
+        w_scales = tiles("w_scales", 1, [NP, REF_PASSES, B], U8)[0]
+        inc_raw = tiles("inc_raw", E_PASSES, [NP, 4, BANK], BF16)
+        inc_in = tiles("inc_in", E_PASSES, [NP, 4 * BANK], BF16)
+        inc_codes = tiles("inc_codes", E_PASSES, [NP, BANK], U32)
+        inc_scales = tiles("inc_scales", E_PASSES, [NP, BANK], U8)
+        r_codes = tiles("r_codes", Y_GROUPS, [NP, E_PASSES, BANK], U32)
+        r_scales = tiles("r_scales", 1, [NP, E_PASSES, P], U8)[0]
+
+        ref_in = tiles("ref_in", 4, [NP, BANK], F32)
+        ref_codes = tiles("ref_codes", 4, [NP, 2 * NP], U32)
+        ref_sc = tiles("ref_sc", 4, [NP, 2 * NP], U8)
+        pl_in = tiles("pl_in", 2, [NP, 2 * NP], F32)
+        pl_codes = tiles("pl_codes", 2, [NP, NP], U32)
+        pl_sc = tiles("pl_sc", 2, [NP, NP], U8)
+        e_bf = tiles("e_bf", 4, [NP, 2 * NP], F32)
+        e_in = tiles("e_in", 2, [NP, BANK], F32)
+        e_codes = tiles("e_codes", 2, [NP, 2 * NP], U32)
+        e_sc = tiles("e_sc", 2, [NP, 2 * NP], U8)
+        y = tiles("y", 3, [NP, P], F32)
+        y_bf = tiles("y_bf", 2 * Y_GROUPS, [NP, 2 * NP], F32)
+        y_in01 = tiles("y_in01", 3, [NP, BANK], F32)
+        y_in2 = tiles("y_in2", 3, [NP, 2 * NP], F32)
+        y_codes = [
+            sb.tile([NP, Y_GROUPS, (hi - lo) * NP], U32, name="y_codes%d" % lo, align_bytes=64)
+            for lo, hi in STORE_RUNS
+        ]
+        y_sc = tiles("y_sc", 1, [NP, Y_GROUPS, S], U8)[0]
+
+        nc.vector.memset(rows[:], 0.0)
+        nc.vector.memset(sw_rows[:], 0.0)
+        nc.vector.memset(w_scales[:].rearrange("p g n -> p (g n)").bitcast(I32), 0)
+        nc.vector.memset(r_scales[:].rearrange("p g n -> p (g n)").bitcast(I32), 0)
+        make_identity(nc, ident[:])
+
+        ref_w = ref_dev.bitcast(F32)
+        placed_w = placed_dev.bitcast(F32)
+        inc_k = placed_inc.rearrange("(p j) n -> p j n", j=4)
+        w_words = ref_words.bitcast(I32)
+        r_words = panel_words.rearrange("g p n t -> p g (n t)").bitcast(I32)
+
+        def load_ref(i):
+            nc.sync.dma_start(out=ref[i][:], in_=ref_w[i * NP:(i + 1) * NP, :])
+
+        def load_placed(pair):
+            src = placed_w[pair * 2 * NP:(pair + 1) * 2 * NP, :].rearrange("(i p) w -> p i w", p=NP)
+            nc.sync.dma_start(out=placed[pair][:], in_=src)
+
+        def load_scales(queue, plane, src):
+            for q in range(4):
+                queue.dma_start(
+                    out=plane[32 * q:32 * q + 4, :, :].bitcast(I32),
+                    in_=src.bitcast(I32)[:, 4 * q:4 * q + 4, :].rearrange("g r w -> r g w"),
+                )
+
+        def word_rows(vec):
+            return vec.rearrange("(m w) -> m w", w=2 * NP).bitcast(F32)
+
+        load_ref(0)
+        nc.scalar.dma_start(out=rows[32:36, :], in_=word_rows(root_length))
+        nc.scalar.dma_start(out=sw_rows[0:TILES, :], in_=sample_weight.rearrange("(i p) -> i p", p=NP))
+        nc.scalar.dma_start(out=rows[36:42, :], in_=word_rows(offset))
+        nc.scalar.dma_start(out=rows[42:48, :], in_=word_rows(panel_weight))
+        load_scales(nc.gpsimd, w_scales, ref_scales)
+        for h in range(E_PASSES):
+            nc.sync.dma_start(out=inc_raw[h][:], in_=inc_k[:, :, h * BANK:(h + 1) * BANK])
+        load_placed(0)
+        for h in range(E_PASSES):
+            src = w_words[:, :, h * 256:(h + 1) * 256].rearrange("g p w -> p g w")
+            nc.sync.dma_start(out=w_codes[h][:].bitcast(I32), in_=src)
+        load_ref(1)
+        load_scales(nc.sync, r_scales, panel_scales)
+        load_ref(2)
+        load_placed(1)
+        for n in range(Y_GROUPS):
+            nc.sync.dma_start(out=r_codes[n][:].bitcast(I32), in_=r_words[:, :, n * BANK:(n + 1) * BANK])
+        for i in range(3, TILES):
+            load_ref(i)
+            if i % 2 == 1 and i + 1 < TILES:
+                load_placed((i + 1) // 2)
+
+        def live(i):
+            return 0 <= i < TILES
+
+        def turn(bank, slot, words):
+            nc.tensor.transpose(bank[:, slot * NP:(slot + 1) * NP], words, ident[:])
+
+        def pair_up(dst, src):
+            nc.scalar.copy(
+                out=dst.rearrange("p (g s u) -> p g s u", u=2, s=NP),
+                in_=src.rearrange("p (g u s) -> p g s u", u=2, s=NP),
+            )
+
+        def quantize(codes, scales, src):
+            nc.vector.quantize_mx(out=codes.bitcast(FP8X4), scales=scales, in_=src.bitcast(BF16))
+
+        def sorted_read(ap):
+            return ap.rearrange("s (p u e) -> s u p e", u=2, e=2)
+
+        def sorted_write(ap):
+            return ap.bitcast(BF16).rearrange("s (u p e) -> s u p e", u=2, e=2)
+
+        def spread(bank, first_row, count):
+            for m in range(count):
+                turn(bank, m, cols[:, first_row + m:first_row + m + 1].to_broadcast([NP, NP]))
+
+        def turn_vectors():
+            nc.vector.tensor_copy(out=rows[0:32, :], in_=sw_rows[:])
+            bank = take_bank()
+            turn(bank, 0, rows[:])
+            nc.scalar.copy(out=cols[:], in_=bank[:, 0:64])
+
+        def spread_root():
+            bank = take_bank()
+            spread(bank, 32, 4)
+            nc.scalar.copy(
+                out=root[:].rearrange("s (g u p) -> s g u p", g=2, u=2),
+                in_=bank[:].rearrange("s (g p u) -> s g u p", g=2, u=2),
+            )
+
+        def spread_panel():
+            for k in range(3):
+                bank = take_bank()
+                spread(bank, 36 + 4 * k, 4)
+                nc.scalar.copy(out=panel[:, k * BANK:(k + 1) * BANK], in_=bank[:])
+
+        def quantize_inc(h):
+            nc.vector.tensor_copy(
+                out=inc_in[h][:].rearrange("p (c i t) -> p c t i", i=4, t=4),
+                in_=inc_raw[h][:].rearrange("p t (c i) -> p c t i", i=4),
+            )
+
+        def quantize_inc2(h):
+            nc.vector.quantize_mx(out=inc_codes[h][:].bitcast(FP8X4), scales=inc_scales[h][:], in_=inc_in[h][:])
+
+        panel_bf = panel[:].bitcast(BF16)
+        root_bf = root[:].bitcast(BF16)
+        e_banks = {}
+        g_banks = {}
+
+        def turn_ref(j):
+            for half in range(2):
+                bank = take_bank()
+                for g in range(2):
+                    for u in range(2):
+                        k0 = 256 * (2 * half + g)
+                        turn(bank, 2 * g + u, ref[j][:, k0 + u:k0 + 256:2])
+                pair_up(ref_in[2 * (j % 2) + half][:], bank[:])
+
+        def quant_ref(j, half):
+            n = 2 * (j % 2) + half
+            quantize(ref_codes[n][:], ref_sc[n][:], ref_in[n][:])
+
+        def embed(j, h):
+            bank = take_bank()
+            e_banks[(j, h)] = bank
+            for g in range(REF_PASSES):
+                n = 2 * (j % 2) + g // 2
+                c = slice((g % 2) * NP, (g % 2 + 1) * NP)
+                nc.tensor.matmul_mx(
+                    out=bank[:], lhsT=ref_codes[n][:, c].bitcast(FP8X4), lhsT_scale=ref_sc[n][:, c],
+                    rhs=w_codes[h][:, g, :].bitcast(FP4X4), rhs_scale=w_scales[:, g, h * BANK:(h + 1) * BANK],
+                    start=(g == 0), stop=False,
+                )
+            nc.tensor.matmul_mx(
+                out=bank[:], lhsT=pl_codes[j % 2][:].bitcast(FP8X4), lhsT_scale=pl_sc[j % 2][:],
+                rhs=inc_codes[h][:].bitcast(FP8X4), rhs_scale=inc_scales[h][:],
+                start=False, stop=True,
+            )
+
+        def scale_e(j, h):
+            nc.vector.tensor_tensor(
+                out=sorted_write(e_bf[2 * (j % 2) + h][:]),
+                in0=sorted_read(e_banks[(j, h)][:]),
+                in1=root_bf[:, h * BANK:(h + 1) * BANK].rearrange("s (u p e) -> s u p e", u=2, e=2),
+                op=MULT,
+            )
+
+        def turn_e(j):
+            bank = take_bank()
+            for g in range(E_PASSES):
+                for u in range(2):
+                    turn(bank, 2 * g + u, e_bf[2 * (j % 2) + g][:, u * NP:(u + 1) * NP])
+            pair_up(e_in[j % 2][:], bank[:])
+
+        def gram(j):
+            for n in range(Y_GROUPS):
+                bank = take_bank()
+                g_banks[(j, n)] = bank
+                for g in range(E_PASSES):
+                    c = slice(g * NP, (g + 1) * NP)
+                    nc.tensor.matmul_mx(
+                        out=bank[:], lhsT=e_codes[j % 2][:, c].bitcast(FP8X4), lhsT_scale=e_sc[j % 2][:, c],
+                        rhs=r_codes[n][:, g, :].bitcast(FP8X4), rhs_scale=r_scales[:, g, n * BANK:(n + 1) * BANK],
+                        start=(g == 0), stop=(g == E_PASSES - 1),
+                    )
+
+        def shift(j, n):
+            c = slice(n * BANK, (n + 1) * BANK)
+            nc.vector.scalar_tensor_tensor(
+                out=y[j % 3][:, c], in0=g_banks[(j, n)][:], scalar=cols[:, j:j + 1], in1=panel_bf[:, c],
+                op0=MULT, op1=ADD,
+            )
+
+        def weigh(j, n):
+            c = slice(n * BANK, (n + 1) * BANK)
+            nc.vector.tensor_tensor(
+                out=y[j % 3][:, c], in0=y[j % 3][:, c], in1=panel_bf[:, P + n * BANK:P + (n + 1) * BANK], op=MULT,
+            )
+
+        def round_y(j, n):
+            nc.scalar.copy(
+                out=sorted_write(y_bf[Y_GROUPS * (j % 2) + n][:]),
+                in_=sorted_read(y[j % 3][:, n * BANK:(n + 1) * BANK]),
+            )
+
+        def turn_y01(j):
+            bank = take_bank()
+            for g in range(2):
+                for u in range(2):
+                    turn(bank, 2 * g + u, y_bf[Y_GROUPS * (j % 2) + g][:, u * NP:(u + 1) * NP])
+            pair_up(y_in01[j % 3][:], bank[:])
+
+        def turn_rest(jy, jp):
+            bank = take_bank()
+            for u in range(2):
+                if live(jy):
+                    turn(bank, u, y_bf[Y_GROUPS * (jy % 2) + 2][:, u * NP:(u + 1) * NP])
+            for u in range(2):
+                if live(jp):
+                    turn(bank, 2 + u, placed[jp // 2][:, jp % 2, u:256:2])
+            return bank
+
+        def pair_rest(bank, jy, jp):
+            if live(jy):
+                pair_up(y_in2[jy % 3][:], bank[:, 0:256])
+            if live(jp):
+                pair_up(pl_in[jp % 2][:], bank[:, 256:512])
+
+        def quant_y(j, groups):
+            run = [r for r, (lo, hi) in enumerate(STORE_RUNS) if lo <= j < hi][0]
+            lo, hi = STORE_RUNS[run]
+            for g in groups:
+                src = y_in01[j % 3][:, g * 256:(g + 1) * 256] if g < 2 else y_in2[j % 3][:]
+                quantize(y_codes[run][:, g, (j - lo) * NP:(j - lo + 1) * NP], y_sc[:, g, j * NP:(j + 1) * NP], src)
+            if j == hi - 1:
+                gs = slice(groups[0], groups[-1] + 1)
+                dst = out_1.rearrange("g p m t -> p g (m t)").bitcast(I32)[:, gs, lo * NP:hi * NP]
+                nc.sync.dma_start(out=dst, in_=y_codes[run][:, gs, :].bitcast(I32))
+
+        def store_y(j, c):
+            nc.sync.dma_start(out=out_0[j * NP:(j + 1) * NP, c], in_=y[j % 3][:, c])
+
+        turn_vectors()
+        quantize_inc(0)
+
+        last = TILES - 1
+        for j in range(TILES + 2):
+            jd, je, jy, jp = j - 2, j - 1, j - 3, j + 1
+            if live(j):
+                turn_ref(j)
+            if j == 0:
+                spread_root()
+                pair_rest(turn_rest(-1, 0), -1, 0)
+                quantize_inc2(0)
+            if live(je):
+                scale_e(je, 1)
+            if live(j) and j > 0:
+                quantize(pl_codes[j % 2][:], pl_sc[j % 2][:], pl_in[j % 2][:])
+            if live(j):
+                quant_ref(j, 0)
+                quant_ref(j, 1)
+            if j == 0:
+                quantize(pl_codes[0][:], pl_sc[0][:], pl_in[0][:])
+                quantize_inc(1)
+                quantize_inc2(1)
+            if live(jd):
+                gram(jd)
+            if live(je):
+                turn_e(je)
+            if j == 1:
+                spread_panel()
+            if live(jy):
+                turn_y01(jy)
+            rest = turn_rest(jy, jp) if live(jy) or live(jp) else None
+            if live(jd):
+                shift(jd, 0)
+                shift(jd, 1)
+                weigh(jd, 0)
+                round_y(jd, 0)
+                if jd == last:
+                    store_y(jd, slice(0, BANK))
+                shift(jd, 2)
+            if rest is not None:
+                pair_rest(rest, jy, jp)
+            if je == last:
+                quantize(e_codes[je % 2][:], e_sc[je % 2][:], e_in[je % 2][:])
+            if live(jd):
+                weigh(jd, 1)
+                round_y(jd, 1)
+                if jd == last:
+                    store_y(jd, slice(BANK, 2 * BANK))
+            if live(je) and je != last:
+                quantize(e_codes[je % 2][:], e_sc[je % 2][:], e_in[je % 2][:])
+            if live(jd):
+                weigh(jd, 2)
+                round_y(jd, 2)
+                store_y(jd, slice(2 * BANK, P) if jd == last else slice(0, P))
+            if live(j):
+                embed(j, 0)
+                embed(j, 1)
+                scale_e(j, 0)
+                if live(jy):
+                    quant_y(jy, [0, 1, 2])
+
+        turn_y01(last)
+        pair_rest(turn_rest(last, -1), last, -1)
+        quant_y(last - 2, [0, 1, 2])
+        quant_y(last - 1, [0, 1, 2])
+        quant_y(last, [0, 1, 2])
+
+        for q in range(4):
+            queue = nc.sync if q % 2 == 0 else nc.scalar
+            queue.dma_start(
+                out=out_2.bitcast(I32)[:, 4 * q:4 * q + 4, :].rearrange("g r w -> r g w"),
+                in_=y_sc[32 * q:32 * q + 4, :, :].bitcast(I32),
+            )

@@ -48,11 +48,12 @@ def tile_community_branch_gram_k6_kernel(
         ident = tiles("ident", 1, [NP, NP], F32)[0]
         rows = tiles("rows", 1, [NP, NP], F32)[0]
         sw_rows = tiles("sw_rows", 1, [32, NP], BF16)[0]
+        root_cols = tiles("root_cols", 1, [NP, 4], F32)[0]
         cols = tiles("cols", 1, [NP, 64], F32)[0]
         root = tiles("root", 1, [NP, B // 2], F32)[0]
         panel = tiles("panel", 1, [NP, P], F32)[0]
         ref = tiles("ref", TILES, [NP, T // 2], F32)
-        placed = tiles("placed", TILES // 2, [NP, 2, V // 2], F32)
+        placed = tiles("placed", TILES, [NP, V // 2], F32)
         w_codes = tiles("w_codes", E_PASSES, [NP, REF_PASSES, 2 * BANK], U8)
         w_scales = tiles("w_scales", 1, [NP, REF_PASSES, B], U8)[0]
         inc_raw = tiles("inc_raw", E_PASSES, [NP, 4, BANK], BF16)
@@ -62,9 +63,9 @@ def tile_community_branch_gram_k6_kernel(
         r_codes = tiles("r_codes", Y_GROUPS, [NP, E_PASSES, BANK], U32)
         r_scales = tiles("r_scales", 1, [NP, E_PASSES, P], U8)[0]
 
-        ref_in = tiles("ref_in", 4, [NP, BANK], F32)
-        ref_codes = tiles("ref_codes", 4, [NP, 2 * NP], U32)
-        ref_sc = tiles("ref_sc", 4, [NP, 2 * NP], U8)
+        ref_in = tiles("ref_in", 2, [NP, 2 * BANK], F32)
+        ref_codes = tiles("ref_codes", 2, [NP, 4 * NP], U32)
+        ref_sc = tiles("ref_sc", 2, [NP, 4 * NP], U8)
         pl_in = tiles("pl_in", 2, [NP, 2 * NP], F32)
         pl_codes = tiles("pl_codes", 2, [NP, NP], U32)
         pl_sc = tiles("pl_sc", 2, [NP, NP], U8)
@@ -82,9 +83,9 @@ def tile_community_branch_gram_k6_kernel(
         ]
         y_sc = tiles("y_sc", 1, [NP, Y_GROUPS, S], U8)[0]
 
+        nc.vector.memset(w_scales[:].rearrange("p g n -> p (g n)").bitcast(I32), 0)
         nc.vector.memset(rows[:], 0.0)
         nc.vector.memset(sw_rows[:], 0.0)
-        nc.vector.memset(w_scales[:].rearrange("p g n -> p (g n)").bitcast(I32), 0)
         nc.vector.memset(r_scales[:].rearrange("p g n -> p (g n)").bitcast(I32), 0)
         make_identity(nc, ident[:])
 
@@ -97,9 +98,15 @@ def tile_community_branch_gram_k6_kernel(
         def load_ref(i):
             nc.sync.dma_start(out=ref[i][:], in_=ref_w[i * NP:(i + 1) * NP, :])
 
-        def load_placed(pair):
-            src = placed_w[pair * 2 * NP:(pair + 1) * 2 * NP, :].rearrange("(i p) w -> p i w", p=NP)
-            nc.sync.dma_start(out=placed[pair][:], in_=src)
+        def load_placed(i):
+            nc.sync.dma_start(out=placed[i][:], in_=placed_w[i * NP:(i + 1) * NP, :])
+
+        def load_w(h):
+            src = w_words[:, :, h * 256:(h + 1) * 256].rearrange("g p w -> p g w")
+            nc.sync.dma_start(out=w_codes[h][:].bitcast(I32), in_=src)
+
+        def load_inc(h):
+            nc.sync.dma_start(out=inc_raw[h][:], in_=inc_k[:, :, h * BANK:(h + 1) * BANK])
 
         def load_scales(queue, plane, src):
             for q in range(4):
@@ -111,28 +118,28 @@ def tile_community_branch_gram_k6_kernel(
         def word_rows(vec):
             return vec.rearrange("(m w) -> m w", w=2 * NP).bitcast(F32)
 
-        load_ref(0)
-        nc.scalar.dma_start(out=rows[32:36, :], in_=word_rows(root_length))
-        nc.scalar.dma_start(out=sw_rows[0:TILES, :], in_=sample_weight.rearrange("(i p) -> i p", p=NP))
-        nc.scalar.dma_start(out=rows[36:42, :], in_=word_rows(offset))
-        nc.scalar.dma_start(out=rows[42:48, :], in_=word_rows(panel_weight))
-        load_scales(nc.gpsimd, w_scales, ref_scales)
-        for h in range(E_PASSES):
-            nc.sync.dma_start(out=inc_raw[h][:], in_=inc_k[:, :, h * BANK:(h + 1) * BANK])
-        load_placed(0)
-        for h in range(E_PASSES):
-            src = w_words[:, :, h * 256:(h + 1) * 256].rearrange("g p w -> p g w")
-            nc.sync.dma_start(out=w_codes[h][:].bitcast(I32), in_=src)
-        load_ref(1)
-        load_scales(nc.sync, r_scales, panel_scales)
-        load_ref(2)
-        load_placed(1)
-        for n in range(Y_GROUPS):
-            nc.sync.dma_start(out=r_codes[n][:].bitcast(I32), in_=r_words[:, :, n * BANK:(n + 1) * BANK])
-        for i in range(3, TILES):
-            load_ref(i)
-            if i % 2 == 1 and i + 1 < TILES:
-                load_placed((i + 1) // 2)
+        def load_all():
+            load_ref(0)
+            nc.sync.dma_start(out=root_cols[:], in_=root_length.rearrange("(p w) -> p w", p=NP).bitcast(F32))
+            nc.gpsimd.dma_start(out=sw_rows[0:TILES, :], in_=sample_weight.rearrange("(i p) -> i p", p=NP))
+            nc.gpsimd.dma_start(out=rows[32:38, :], in_=word_rows(offset))
+            nc.gpsimd.dma_start(out=rows[38:44, :], in_=word_rows(panel_weight))
+            load_w(0)
+            load_scales(nc.sync, w_scales, ref_scales)
+            load_placed(0)
+            load_inc(0)
+            load_ref(1)
+            load_placed(1)
+            load_inc(1)
+            load_w(1)
+            load_ref(2)
+            load_placed(2)
+            load_scales(nc.sync, r_scales, panel_scales)
+            for n in range(Y_GROUPS):
+                nc.sync.dma_start(out=r_codes[n][:].bitcast(I32), in_=r_words[:, :, n * BANK:(n + 1) * BANK])
+            for i in range(3, TILES):
+                load_ref(i)
+                load_placed(i)
 
         def live(i):
             return 0 <= i < TILES
@@ -155,29 +162,27 @@ def tile_community_branch_gram_k6_kernel(
         def sorted_write(ap):
             return ap.bitcast(BF16).rearrange("s (u p e) -> s u p e", u=2, e=2)
 
-        def spread(bank, first_row, count):
-            for m in range(count):
-                turn(bank, m, cols[:, first_row + m:first_row + m + 1].to_broadcast([NP, NP]))
+        def spread(bank, src, first):
+            for m in range(4):
+                turn(bank, m, src[:, first + m:first + m + 1].to_broadcast([NP, NP]))
 
         def turn_vectors():
-            nc.vector.tensor_copy(out=rows[0:32, :], in_=sw_rows[:])
             bank = take_bank()
             turn(bank, 0, rows[:])
             nc.scalar.copy(out=cols[:], in_=bank[:, 0:64])
 
         def spread_root():
             bank = take_bank()
-            spread(bank, 32, 4)
+            spread(bank, root_cols, 0)
             nc.scalar.copy(
-                out=root[:].rearrange("s (g u p) -> s g u p", g=2, u=2),
-                in_=bank[:].rearrange("s (g p u) -> s g u p", g=2, u=2),
+                out=root[:].rearrange("s (g u h b) -> s g u h b", g=2, u=2, b=2),
+                in_=bank[:].rearrange("s (b u g h) -> s g u h b", g=2, u=2, b=2),
             )
 
-        def spread_panel():
-            for k in range(3):
-                bank = take_bank()
-                spread(bank, 36 + 4 * k, 4)
-                nc.scalar.copy(out=panel[:, k * BANK:(k + 1) * BANK], in_=bank[:])
+        def spread_panel(k):
+            bank = take_bank()
+            spread(bank, cols, 32 + 4 * k)
+            nc.scalar.copy(out=panel[:, k * BANK:(k + 1) * BANK], in_=bank[:])
 
         def quantize_inc(h):
             nc.vector.tensor_copy(
@@ -200,18 +205,18 @@ def tile_community_branch_gram_k6_kernel(
                     for u in range(2):
                         k0 = 256 * (2 * half + g)
                         turn(bank, 2 * g + u, ref[j][:, k0 + u:k0 + 256:2])
-                pair_up(ref_in[2 * (j % 2) + half][:], bank[:])
+                pair_up(ref_in[j % 2][:, half * BANK:(half + 1) * BANK], bank[:])
 
-        def quant_ref(j, half):
-            n = 2 * (j % 2) + half
-            quantize(ref_codes[n][:], ref_sc[n][:], ref_in[n][:])
+        def quant_ref(j, lo, hi):
+            c = slice(lo * NP, hi * NP)
+            quantize(ref_codes[j % 2][:, c], ref_sc[j % 2][:, c], ref_in[j % 2][:, lo * 256:hi * 256])
 
         def embed(j, h):
             bank = take_bank()
             e_banks[(j, h)] = bank
             for g in range(REF_PASSES):
-                n = 2 * (j % 2) + g // 2
-                c = slice((g % 2) * NP, (g % 2 + 1) * NP)
+                n = j % 2
+                c = slice(g * NP, (g + 1) * NP)
                 nc.tensor.matmul_mx(
                     out=bank[:], lhsT=ref_codes[n][:, c].bitcast(FP8X4), lhsT_scale=ref_sc[n][:, c],
                     rhs=w_codes[h][:, g, :].bitcast(FP4X4), rhs_scale=w_scales[:, g, h * BANK:(h + 1) * BANK],
@@ -238,8 +243,8 @@ def tile_community_branch_gram_k6_kernel(
                     turn(bank, 2 * g + u, e_bf[2 * (j % 2) + g][:, u * NP:(u + 1) * NP])
             pair_up(e_in[j % 2][:], bank[:])
 
-        def gram(j):
-            for n in range(Y_GROUPS):
+        def gram(j, groups):
+            for n in groups:
                 bank = take_bank()
                 g_banks[(j, n)] = bank
                 for g in range(E_PASSES):
@@ -257,9 +262,9 @@ def tile_community_branch_gram_k6_kernel(
                 op0=MULT, op1=ADD,
             )
 
-        def weigh(j, n):
+        def weigh(engine, j, n):
             c = slice(n * BANK, (n + 1) * BANK)
-            nc.vector.tensor_tensor(
+            engine.tensor_tensor(
                 out=y[j % 3][:, c], in0=y[j % 3][:, c], in1=panel_bf[:, P + n * BANK:P + (n + 1) * BANK], op=MULT,
             )
 
@@ -283,7 +288,7 @@ def tile_community_branch_gram_k6_kernel(
                     turn(bank, u, y_bf[Y_GROUPS * (jy % 2) + 2][:, u * NP:(u + 1) * NP])
             for u in range(2):
                 if live(jp):
-                    turn(bank, 2 + u, placed[jp // 2][:, jp % 2, u:256:2])
+                    turn(bank, 2 + u, placed[jp][:, u:256:2])
             return bank
 
         def pair_rest(bank, jy, jp):
@@ -306,68 +311,92 @@ def tile_community_branch_gram_k6_kernel(
         def store_y(j, c):
             nc.sync.dma_start(out=out_0[j * NP:(j + 1) * NP, c], in_=y[j % 3][:, c])
 
-        turn_vectors()
+        def quant_placed(j):
+            quantize(pl_codes[j % 2][:], pl_sc[j % 2][:], pl_in[j % 2][:])
+
+        def quant_e(j):
+            quantize(e_codes[j % 2][:], e_sc[j % 2][:], e_in[j % 2][:])
+
+        load_all()
+        turn_ref(0)
+        pair_rest(turn_rest(-1, 0), -1, 0)
+        spread_root()
+        quant_ref(0, 0, 2)
+        quant_ref(0, 2, 4)
+        nc.vector.tensor_copy(out=rows[0:32, :], in_=sw_rows[:])
         quantize_inc(0)
+        quant_placed(0)
+        quantize_inc2(0)
+        embed(0, 0)
 
         last = TILES - 1
-        for j in range(TILES + 2):
-            jd, je, jy, jp = j - 2, j - 1, j - 3, j + 1
-            if live(j):
-                turn_ref(j)
+        for j in range(TILES):
+            jx, jd, jy, jp = j + 1, j - 1, j - 2, j + 2
+            scale_e(j, 0)
+            if live(j - 3):
+                quant_y(j - 3, [0, 1, 2])
             if j == 0:
-                spread_root()
-                pair_rest(turn_rest(-1, 0), -1, 0)
-                quantize_inc2(0)
-            if live(je):
-                scale_e(je, 1)
-            if live(j) and j > 0:
-                quantize(pl_codes[j % 2][:], pl_sc[j % 2][:], pl_in[j % 2][:])
-            if live(j):
-                quant_ref(j, 0)
-                quant_ref(j, 1)
-            if j == 0:
-                quantize(pl_codes[0][:], pl_sc[0][:], pl_in[0][:])
+                pair_rest(turn_rest(-1, 1), -1, 1)
                 quantize_inc(1)
+            if live(jx):
+                turn_ref(jx)
+            if j == 0:
+                turn_vectors()
                 quantize_inc2(1)
-            if live(jd):
-                gram(jd)
-            if live(je):
-                turn_e(je)
-            if j == 1:
-                spread_panel()
+            if live(jy):
+                round_y(jy, 1)
+                round_y(jy, 2)
+            if live(jx):
+                quant_placed(jx)
+                quant_ref(jx, 0, 4)
+            embed(j, 1)
+            scale_e(j, 1)
+            if j == last:
+                gram(jd, [0])
+                turn_e(j)
+                gram(jd, [1, 2])
+            else:
+                if live(jd):
+                    gram(jd, [0, 1, 2])
+                if j == 0:
+                    spread_panel(0)
+                    spread_panel(1)
+                if j == 1:
+                    spread_panel(2)
+                turn_e(j)
             if live(jy):
                 turn_y01(jy)
-            rest = turn_rest(jy, jp) if live(jy) or live(jp) else None
+            if live(jy) or live(jp):
+                pair_rest(turn_rest(jy, jp), jy, jp)
             if live(jd):
                 shift(jd, 0)
+                weigh(nc.gpsimd, jd, 0)
                 shift(jd, 1)
-                weigh(jd, 0)
                 round_y(jd, 0)
-                if jd == last:
-                    store_y(jd, slice(0, BANK))
+                if j == last:
+                    quant_e(j)
                 shift(jd, 2)
-            if rest is not None:
-                pair_rest(rest, jy, jp)
-            if je == last:
-                quantize(e_codes[je % 2][:], e_sc[je % 2][:], e_in[je % 2][:])
-            if live(jd):
-                weigh(jd, 1)
-                round_y(jd, 1)
-                if jd == last:
-                    store_y(jd, slice(BANK, 2 * BANK))
-            if live(je) and je != last:
-                quantize(e_codes[je % 2][:], e_sc[je % 2][:], e_in[je % 2][:])
-            if live(jd):
-                weigh(jd, 2)
-                round_y(jd, 2)
-                store_y(jd, slice(2 * BANK, P) if jd == last else slice(0, P))
-            if live(j):
-                embed(j, 0)
-                embed(j, 1)
-                scale_e(j, 0)
-                if live(jy):
-                    quant_y(jy, [0, 1, 2])
+                weigh(nc.vector, jd, 1)
+                weigh(nc.gpsimd, jd, 2)
+                store_y(jd, slice(0, P))
+            if j != last:
+                quant_e(j)
+                embed(jx, 0)
 
+        round_y(last - 1, 1)
+        round_y(last - 1, 2)
+        gram(last, [0, 1, 2])
+        turn_y01(last - 1)
+        pair_rest(turn_rest(last - 1, -1), last - 1, -1)
+        shift(last, 0)
+        shift(last, 1)
+        weigh(nc.gpsimd, last, 0)
+        shift(last, 2)
+        for n in range(Y_GROUPS):
+            if n > 0:
+                weigh(nc.vector, last, n)
+            round_y(last, n)
+            store_y(last, slice(n * BANK, (n + 1) * BANK))
         turn_y01(last)
         pair_rest(turn_rest(last, -1), last, -1)
         quant_y(last - 2, [0, 1, 2])

@@ -22,7 +22,10 @@ TILES = S // NP
 REF_PASSES = T // 512
 E_PASSES = B // 512
 Y_GROUPS = P // 512
-STORE_RUNS = [(0, 1), (1, 3), (3, 5), (5, 7), (7, 8)]
+FIRST_SORTED = 3
+INC_SPLIT = 352
+SCALE_RUNS = [(0, 6), (6, 8)]
+STORE_RUNS = [(0, 2), (2, 4), (4, 6), (6, 7), (7, 8)]
 
 
 def tile_community_branch_gram_k6_kernel(
@@ -39,11 +42,12 @@ def tile_community_branch_gram_k6_kernel(
             return [sb.tile(shape, dtype, name="%s%d" % (name, i), align_bytes=64) for i in range(count)]
 
         banks = [ps.tile([NP, BANK], F32, name="bank%d" % i) for i in range(8)]
-        taken = []
+        free = list(range(len(banks)))
 
         def take_bank():
-            taken.append(0)
-            return banks[(len(taken) - 1) % len(banks)]
+            index = free[0]
+            free.remove(index)
+            return index
 
         ident = tiles("ident", 1, [NP, NP], F32)[0]
         rows = tiles("rows", 1, [NP, NP], F32)[0]
@@ -52,17 +56,20 @@ def tile_community_branch_gram_k6_kernel(
         cols = tiles("cols", 1, [NP, 64], F32)[0]
         root = tiles("root", 1, [NP, B // 2], F32)[0]
         panel = tiles("panel", 1, [NP, P], F32)[0]
-        ref = tiles("ref", TILES, [NP, T // 2], F32)
+        ref = [None] + tiles("ref", TILES - 1, [NP, T // 2], F32)
+        ref_first = tiles("ref_first", 2, [NP, T // 4], F32)
         placed = tiles("placed", TILES, [NP, V // 2], F32)
-        w_codes = tiles("w_codes", E_PASSES, [NP, REF_PASSES, 2 * BANK], U8)
+        w_codes = tiles("w_codes", REF_PASSES // 2, [NP, 2, 2 * B], U8)
         w_scales = tiles("w_scales", 1, [NP, REF_PASSES, B], U8)[0]
-        inc_raw = tiles("inc_raw", E_PASSES, [NP, 4, BANK], BF16)
+        inc_raw = tiles("inc_raw", 1, [NP, 4, B], BF16)[0]
         inc_in = tiles("inc_in", E_PASSES, [NP, 4 * BANK], BF16)
         inc_codes = tiles("inc_codes", E_PASSES, [NP, BANK], U32)
         inc_scales = tiles("inc_scales", E_PASSES, [NP, BANK], U8)
         r_codes = tiles("r_codes", Y_GROUPS, [NP, E_PASSES, BANK], U32)
         r_scales = tiles("r_scales", 1, [NP, E_PASSES, P], U8)[0]
 
+        ref_sorted = tiles("ref_sorted", 2, [NP, T // 2], F32)
+        pl_sorted = tiles("pl_sorted", 2, [NP, V // 2], F32)
         ref_in = tiles("ref_in", 2, [NP, 2 * BANK], F32)
         ref_codes = tiles("ref_codes", 2, [NP, 4 * NP], U32)
         ref_sc = tiles("ref_sc", 2, [NP, 4 * NP], U8)
@@ -81,7 +88,9 @@ def tile_community_branch_gram_k6_kernel(
             sb.tile([NP, Y_GROUPS, (hi - lo) * NP], U32, name="y_codes%d" % lo, align_bytes=64)
             for lo, hi in STORE_RUNS
         ]
-        y_sc = tiles("y_sc", 1, [NP, Y_GROUPS, S], U8)[0]
+        y_sc = [
+            sb.tile([NP, Y_GROUPS, (hi - lo) * NP], U8, name="y_sc%d" % lo, align_bytes=64) for lo, hi in SCALE_RUNS
+        ]
 
         nc.vector.memset(w_scales[:].rearrange("p g n -> p (g n)").bitcast(I32), 0)
         nc.vector.memset(rows[:], 0.0)
@@ -102,39 +111,37 @@ def tile_community_branch_gram_k6_kernel(
             nc.sync.dma_start(out=placed[i][:], in_=placed_w[i * NP:(i + 1) * NP, :])
 
         def load_w(h):
-            src = w_words[:, :, h * 256:(h + 1) * 256].rearrange("g p w -> p g w")
+            src = w_words[2 * h:2 * h + 2, :, :].rearrange("g p w -> p g w")
             nc.sync.dma_start(out=w_codes[h][:].bitcast(I32), in_=src)
 
-        def load_inc(h):
-            nc.sync.dma_start(out=inc_raw[h][:], in_=inc_k[:, :, h * BANK:(h + 1) * BANK])
-
-        def load_scales(queue, plane, src):
+        def load_scales(plane, src, passes):
             for q in range(4):
-                queue.dma_start(
-                    out=plane[32 * q:32 * q + 4, :, :].bitcast(I32),
-                    in_=src.bitcast(I32)[:, 4 * q:4 * q + 4, :].rearrange("g r w -> r g w"),
+                nc.sync.dma_start(
+                    out=plane[32 * q:32 * q + 4, passes, :].bitcast(I32),
+                    in_=src.bitcast(I32)[passes, 4 * q:4 * q + 4, :].rearrange("g r w -> r g w"),
                 )
 
         def word_rows(vec):
             return vec.rearrange("(m w) -> m w", w=2 * NP).bitcast(F32)
 
         def load_all():
-            load_ref(0)
+            for half in range(2):
+                nc.sync.dma_start(out=ref_first[half][:], in_=ref_w[0:NP, half * BANK:(half + 1) * BANK])
             nc.sync.dma_start(out=root_cols[:], in_=root_length.rearrange("(p w) -> p w", p=NP).bitcast(F32))
             nc.gpsimd.dma_start(out=sw_rows[0:TILES, :], in_=sample_weight.rearrange("(i p) -> i p", p=NP))
             nc.gpsimd.dma_start(out=rows[32:38, :], in_=word_rows(offset))
             nc.gpsimd.dma_start(out=rows[38:44, :], in_=word_rows(panel_weight))
+            load_scales(w_scales, ref_scales, slice(0, 2))
             load_w(0)
-            load_scales(nc.sync, w_scales, ref_scales)
-            load_placed(0)
-            load_inc(0)
             load_ref(1)
-            load_placed(1)
-            load_inc(1)
+            load_scales(w_scales, ref_scales, slice(2, 4))
             load_w(1)
+            load_placed(0)
+            load_placed(1)
+            nc.sync.dma_start(out=inc_raw[:], in_=inc_k)
             load_ref(2)
             load_placed(2)
-            load_scales(nc.sync, r_scales, panel_scales)
+            load_scales(r_scales, panel_scales, slice(0, 2))
             for n in range(Y_GROUPS):
                 nc.sync.dma_start(out=r_codes[n][:].bitcast(I32), in_=r_words[:, :, n * BANK:(n + 1) * BANK])
             for i in range(3, TILES):
@@ -145,7 +152,7 @@ def tile_community_branch_gram_k6_kernel(
             return 0 <= i < TILES
 
         def turn(bank, slot, words):
-            nc.tensor.transpose(bank[:, slot * NP:(slot + 1) * NP], words, ident[:])
+            nc.tensor.transpose(banks[bank][:, slot * NP:(slot + 1) * NP], words, ident[:])
 
         def pair_up(dst, src):
             nc.scalar.copy(
@@ -169,25 +176,34 @@ def tile_community_branch_gram_k6_kernel(
         def turn_vectors():
             bank = take_bank()
             turn(bank, 0, rows[:])
-            nc.scalar.copy(out=cols[:], in_=bank[:, 0:64])
+            nc.scalar.copy(out=cols[:], in_=banks[bank][:, 0:64])
+            free.append(bank)
 
         def spread_root():
             bank = take_bank()
             spread(bank, root_cols, 0)
             nc.scalar.copy(
                 out=root[:].rearrange("s (g u h b) -> s g u h b", g=2, u=2, b=2),
-                in_=bank[:].rearrange("s (b u g h) -> s g u h b", g=2, u=2, b=2),
+                in_=banks[bank][:].rearrange("s (b u g h) -> s g u h b", g=2, u=2, b=2),
             )
+            free.append(bank)
 
         def spread_panel(k):
             bank = take_bank()
             spread(bank, cols, 32 + 4 * k)
-            nc.scalar.copy(out=panel[:, k * BANK:(k + 1) * BANK], in_=bank[:])
+            nc.scalar.copy(out=panel[:, k * BANK:(k + 1) * BANK], in_=banks[bank][:])
+            free.append(bank)
 
-        def quantize_inc(h):
-            nc.vector.tensor_copy(
-                out=inc_in[h][:].rearrange("p (c i t) -> p c t i", i=4, t=4),
-                in_=inc_raw[h][:].rearrange("p t (c i) -> p c t i", i=4),
+        def quantize_inc(h, engine_copy, lo, hi):
+            engine_copy(
+                out=inc_in[h][:, 4 * lo:4 * hi].rearrange("p (c i t) -> p c t i", i=4, t=4),
+                in_=inc_raw[:, :, h * BANK + lo:h * BANK + hi].rearrange("p t (c i) -> p c t i", i=4),
+            )
+
+        def sort_words(engine_copy, dst, src):
+            engine_copy(
+                out=dst.rearrange("s (g u p) -> s g u p", u=2, p=NP),
+                in_=src.rearrange("s (g p u) -> s g u p", u=2, p=NP),
             )
 
         def quantize_inc2(h):
@@ -204,63 +220,84 @@ def tile_community_branch_gram_k6_kernel(
                 for g in range(2):
                     for u in range(2):
                         k0 = 256 * (2 * half + g)
-                        turn(bank, 2 * g + u, ref[j][:, k0 + u:k0 + 256:2])
-                pair_up(ref_in[j % 2][:, half * BANK:(half + 1) * BANK], bank[:])
+                        if j == 0:
+                            words = ref_first[half][:, 256 * g + u:256 * (g + 1):2]
+                        elif j < FIRST_SORTED:
+                            words = ref[j][:, k0 + u:k0 + 256:2]
+                        else:
+                            words = ref_sorted[j % 2][:, k0 + u * NP:k0 + (u + 1) * NP]
+                        turn(bank, 2 * g + u, words)
+                pair_up(ref_in[j % 2][:, half * BANK:(half + 1) * BANK], banks[bank][:])
+                free.append(bank)
 
         def quant_ref(j, lo, hi):
             c = slice(lo * NP, hi * NP)
             quantize(ref_codes[j % 2][:, c], ref_sc[j % 2][:, c], ref_in[j % 2][:, lo * 256:hi * 256])
 
-        def embed(j, h):
-            bank = take_bank()
-            e_banks[(j, h)] = bank
-            for g in range(REF_PASSES):
-                n = j % 2
+        def embed_ref(j, h, passes):
+            for g in passes:
+                if g == 0:
+                    e_banks[(j, h)] = take_bank()
                 c = slice(g * NP, (g + 1) * NP)
                 nc.tensor.matmul_mx(
-                    out=bank[:], lhsT=ref_codes[n][:, c].bitcast(FP8X4), lhsT_scale=ref_sc[n][:, c],
-                    rhs=w_codes[h][:, g, :].bitcast(FP4X4), rhs_scale=w_scales[:, g, h * BANK:(h + 1) * BANK],
+                    out=banks[e_banks[(j, h)]][:],
+                    lhsT=ref_codes[j % 2][:, c].bitcast(FP8X4), lhsT_scale=ref_sc[j % 2][:, c],
+                    rhs=w_codes[g // 2][:, g % 2, 2 * h * BANK:2 * (h + 1) * BANK].bitcast(FP4X4),
+                    rhs_scale=w_scales[:, g, h * BANK:(h + 1) * BANK],
                     start=(g == 0), stop=False,
                 )
+
+        def embed_placed(j, h):
             nc.tensor.matmul_mx(
-                out=bank[:], lhsT=pl_codes[j % 2][:].bitcast(FP8X4), lhsT_scale=pl_sc[j % 2][:],
+                out=banks[e_banks[(j, h)]][:], lhsT=pl_codes[j % 2][:].bitcast(FP8X4), lhsT_scale=pl_sc[j % 2][:],
                 rhs=inc_codes[h][:].bitcast(FP8X4), rhs_scale=inc_scales[h][:],
                 start=False, stop=True,
             )
 
+        def embed(j, h):
+            embed_ref(j, h, range(REF_PASSES))
+            embed_placed(j, h)
+
         def scale_e(j, h):
             nc.vector.tensor_tensor(
                 out=sorted_write(e_bf[2 * (j % 2) + h][:]),
-                in0=sorted_read(e_banks[(j, h)][:]),
+                in0=sorted_read(banks[e_banks[(j, h)]][:]),
                 in1=root_bf[:, h * BANK:(h + 1) * BANK].rearrange("s (u p e) -> s u p e", u=2, e=2),
                 op=MULT,
             )
+            free.append(e_banks[(j, h)])
 
-        def turn_e(j):
+        def turn_e(j, passes=(0, 1)):
             bank = take_bank()
-            for g in range(E_PASSES):
+            for g in passes:
                 for u in range(2):
                     turn(bank, 2 * g + u, e_bf[2 * (j % 2) + g][:, u * NP:(u + 1) * NP])
-            pair_up(e_in[j % 2][:], bank[:])
+            c = slice(passes[0] * 256, (passes[-1] + 1) * 256)
+            pair_up(e_in[j % 2][:, c], banks[bank][:, c])
+            free.append(bank)
+
+        def gram_pass(j, n, g):
+            if g == 0:
+                g_banks[(j, n)] = take_bank()
+            c = slice(g * NP, (g + 1) * NP)
+            nc.tensor.matmul_mx(
+                out=banks[g_banks[(j, n)]][:], lhsT=e_codes[j % 2][:, c].bitcast(FP8X4), lhsT_scale=e_sc[j % 2][:, c],
+                rhs=r_codes[n][:, g, :].bitcast(FP8X4), rhs_scale=r_scales[:, g, n * BANK:(n + 1) * BANK],
+                start=(g == 0), stop=(g == E_PASSES - 1),
+            )
 
         def gram(j, groups):
             for n in groups:
-                bank = take_bank()
-                g_banks[(j, n)] = bank
                 for g in range(E_PASSES):
-                    c = slice(g * NP, (g + 1) * NP)
-                    nc.tensor.matmul_mx(
-                        out=bank[:], lhsT=e_codes[j % 2][:, c].bitcast(FP8X4), lhsT_scale=e_sc[j % 2][:, c],
-                        rhs=r_codes[n][:, g, :].bitcast(FP8X4), rhs_scale=r_scales[:, g, n * BANK:(n + 1) * BANK],
-                        start=(g == 0), stop=(g == E_PASSES - 1),
-                    )
+                    gram_pass(j, n, g)
 
         def shift(j, n):
             c = slice(n * BANK, (n + 1) * BANK)
             nc.vector.scalar_tensor_tensor(
-                out=y[j % 3][:, c], in0=g_banks[(j, n)][:], scalar=cols[:, j:j + 1], in1=panel_bf[:, c],
+                out=y[j % 3][:, c], in0=banks[g_banks[(j, n)]][:], scalar=cols[:, j:j + 1], in1=panel_bf[:, c],
                 op0=MULT, op1=ADD,
             )
+            free.append(g_banks[(j, n)])
 
         def weigh(engine, j, n):
             c = slice(n * BANK, (n + 1) * BANK)
@@ -268,10 +305,17 @@ def tile_community_branch_gram_k6_kernel(
                 out=y[j % 3][:, c], in0=y[j % 3][:, c], in1=panel_bf[:, P + n * BANK:P + (n + 1) * BANK], op=MULT,
             )
 
-        def round_y(j, n):
-            nc.scalar.copy(
+        def round_y(j, n, engine_copy=nc.scalar.copy):
+            engine_copy(
                 out=sorted_write(y_bf[Y_GROUPS * (j % 2) + n][:]),
                 in_=sorted_read(y[j % 3][:, n * BANK:(n + 1) * BANK]),
+            )
+
+        def weigh_rounded(j, n):
+            c = slice(n * BANK, (n + 1) * BANK)
+            nc.vector.tensor_tensor(
+                out=sorted_write(y_bf[Y_GROUPS * (j % 2) + n][:]), in0=sorted_read(y[j % 3][:, c]),
+                in1=sorted_read(panel_bf[:, P + n * BANK:P + (n + 1) * BANK]), op=MULT,
             )
 
         def turn_y01(j):
@@ -279,34 +323,48 @@ def tile_community_branch_gram_k6_kernel(
             for g in range(2):
                 for u in range(2):
                     turn(bank, 2 * g + u, y_bf[Y_GROUPS * (j % 2) + g][:, u * NP:(u + 1) * NP])
-            pair_up(y_in01[j % 3][:], bank[:])
+            pair_up(y_in01[j % 3][:], banks[bank][:])
+            free.append(bank)
 
-        def turn_rest(jy, jp):
+        def turn_halves(jy, placed_tiles):
             bank = take_bank()
-            for u in range(2):
-                if live(jy):
-                    turn(bank, u, y_bf[Y_GROUPS * (jy % 2) + 2][:, u * NP:(u + 1) * NP])
-            for u in range(2):
-                if live(jp):
-                    turn(bank, 2 + u, placed[jp][:, u:256:2])
-            return bank
-
-        def pair_rest(bank, jy, jp):
+            halves = []
             if live(jy):
-                pair_up(y_in2[jy % 3][:], bank[:, 0:256])
-            if live(jp):
-                pair_up(pl_in[jp % 2][:], bank[:, 256:512])
+                src = y_bf[Y_GROUPS * (jy % 2) + 2]
+                halves.append((y_in2[jy % 3], [src[:, u * NP:(u + 1) * NP] for u in range(2)]))
+            for jp in placed_tiles:
+                if jp < FIRST_SORTED:
+                    halves.append((pl_in[jp % 2], [placed[jp][:, u:256:2] for u in range(2)]))
+                elif live(jp):
+                    halves.append((pl_in[jp % 2], [pl_sorted[jp % 2][:, u * NP:(u + 1) * NP] for u in range(2)]))
+            for k, (dst, words) in enumerate(halves):
+                for u in range(2):
+                    turn(bank, 2 * k + u, words[u])
+            for k, (dst, words) in enumerate(halves):
+                pair_up(dst[:], banks[bank][:, k * 256:(k + 1) * 256])
+            free.append(bank)
 
         def quant_y(j, groups):
             run = [r for r, (lo, hi) in enumerate(STORE_RUNS) if lo <= j < hi][0]
             lo, hi = STORE_RUNS[run]
+            srun = [r for r, (slo, shi) in enumerate(SCALE_RUNS) if slo <= j < shi][0]
+            slo, shi = SCALE_RUNS[srun]
             for g in groups:
                 src = y_in01[j % 3][:, g * 256:(g + 1) * 256] if g < 2 else y_in2[j % 3][:]
-                quantize(y_codes[run][:, g, (j - lo) * NP:(j - lo + 1) * NP], y_sc[:, g, j * NP:(j + 1) * NP], src)
+                quantize(
+                    y_codes[run][:, g, (j - lo) * NP:(j - lo + 1) * NP],
+                    y_sc[srun][:, g, (j - slo) * NP:(j - slo + 1) * NP], src,
+                )
             if j == hi - 1:
-                gs = slice(groups[0], groups[-1] + 1)
-                dst = out_1.rearrange("g p m t -> p g (m t)").bitcast(I32)[:, gs, lo * NP:hi * NP]
-                nc.sync.dma_start(out=dst, in_=y_codes[run][:, gs, :].bitcast(I32))
+                dst = out_1.rearrange("g p m t -> p g (m t)").bitcast(I32)[:, :, lo * NP:hi * NP]
+                nc.sync.dma_start(out=dst, in_=y_codes[run][:].bitcast(I32))
+            if j == shi - 1:
+                for q in range(4):
+                    queue = nc.scalar if j == TILES - 1 and q % 2 == 1 else nc.sync
+                    dst = out_2.bitcast(I32)[:, 4 * q:4 * q + 4, slo * NP // 4:shi * NP // 4]
+                    queue.dma_start(
+                        out=dst.rearrange("g r w -> r g w"), in_=y_sc[srun][32 * q:32 * q + 4, :, :].bitcast(I32),
+                    )
 
         def store_y(j, c):
             nc.sync.dma_start(out=out_0[j * NP:(j + 1) * NP, c], in_=y[j % 3][:, c])
@@ -314,98 +372,158 @@ def tile_community_branch_gram_k6_kernel(
         def quant_placed(j):
             quantize(pl_codes[j % 2][:], pl_sc[j % 2][:], pl_in[j % 2][:])
 
-        def quant_e(j):
-            quantize(e_codes[j % 2][:], e_sc[j % 2][:], e_in[j % 2][:])
+        def quant_e(j, lo=0, hi=2):
+            c = slice(lo * NP, hi * NP)
+            quantize(e_codes[j % 2][:, c], e_sc[j % 2][:, c], e_in[j % 2][:, lo * 256:hi * 256])
+
+        def turn_y(j, n):
+            bank = take_bank()
+            for u in range(2):
+                turn(bank, u, y_bf[Y_GROUPS * (j % 2) + n][:, u * NP:(u + 1) * NP])
+            dst = y_in01[j % 3][:, n * 256:(n + 1) * 256] if n < 2 else y_in2[j % 3][:]
+            pair_up(dst, banks[bank][:, 0:256])
+            free.append(bank)
+
+        def sort_tile(j):
+            sort_words(nc.scalar.copy, pl_sorted[j % 2][:], placed[j][:])
+            sort_words(nc.scalar.copy, ref_sorted[j % 2][:], ref[j][:])
+
+        def interleave_inc(h):
+            quantize_inc(h, nc.vector.tensor_copy, 0, INC_SPLIT)
+            quantize_inc(h, nc.scalar.copy, INC_SPLIT, BANK)
+
+        def finish_y(j, je=None):
+            shift(j, 0)
+            weigh(nc.gpsimd, j, 0)
+            shift(j, 1)
+            shift(j, 2)
+            if je is not None:
+                quant_e(je)
+            weigh(nc.vector, j, 1)
+            weigh(nc.vector, j, 2)
+            store_y(j, slice(0, P))
 
         load_all()
         turn_ref(0)
-        pair_rest(turn_rest(-1, 0), -1, 0)
         spread_root()
         quant_ref(0, 0, 2)
         quant_ref(0, 2, 4)
         nc.vector.tensor_copy(out=rows[0:32, :], in_=sw_rows[:])
-        quantize_inc(0)
-        quant_placed(0)
+        embed_ref(0, 0, [0, 1])
+        embed_ref(0, 1, [0, 1])
+        turn_ref(1)
+        quant_ref(1, 0, 2)
+        quant_ref(1, 2, 4)
+        embed_ref(0, 0, [2, 3])
+        embed_ref(0, 1, [2, 3])
+        interleave_inc(0)
+        interleave_inc(1)
+        turn_halves(-1, [0, 1])
+        turn_vectors()
         quantize_inc2(0)
-        embed(0, 0)
+        quant_placed(0)
+        quantize_inc2(1)
+        quant_placed(1)
+        embed_ref(1, 0, range(REF_PASSES))
+        turn_ref(2)
+        turn_halves(-1, [2])
+        embed_ref(1, 1, range(REF_PASSES))
+        for j in range(2):
+            for h in range(E_PASSES):
+                embed_placed(j, h)
+        quant_ref(2, 0, 4)
+        scale_e(0, 0)
+        scale_e(0, 1)
+        quant_placed(2)
+        spread_panel(0)
+        turn_e(0)
+        spread_panel(1)
+        spread_panel(2)
+        scale_e(1, 0)
+        quant_e(0)
+        scale_e(1, 1)
+        embed(2, 0)
+        gram(0, [0, 1, 2])
+        sort_tile(3)
+        scale_e(2, 0)
+        turn_e(1)
+        finish_y(0, 1)
 
         last = TILES - 1
-        for j in range(TILES):
+        for j in range(2, last):
             jx, jd, jy, jp = j + 1, j - 1, j - 2, j + 2
-            scale_e(j, 0)
+            if j > 2:
+                scale_e(j, 0)
             if live(j - 3):
                 quant_y(j - 3, [0, 1, 2])
-            if j == 0:
-                pair_rest(turn_rest(-1, 1), -1, 1)
-                quantize_inc(1)
-            if live(jx):
-                turn_ref(jx)
-            if j == 0:
-                turn_vectors()
-                quantize_inc2(1)
-            if live(jy):
-                round_y(jy, 1)
-                round_y(jy, 2)
-            if live(jx):
-                quant_placed(jx)
-                quant_ref(jx, 0, 4)
+            turn_ref(jx)
+            if j == 2:
+                turn_halves(-1, [jx])
+                round_y(0, 0)
+            round_y(jy, 1)
+            round_y(jy, 2)
+            if live(jp):
+                sort_tile(jp)
+            quant_placed(jx)
+            quant_ref(jx, 0, 4)
             embed(j, 1)
             scale_e(j, 1)
-            if j == last:
-                gram(jd, [0])
-                turn_e(j)
-                gram(jd, [1, 2])
-            else:
-                if live(jd):
-                    gram(jd, [0, 1, 2])
-                if j == 0:
-                    spread_panel(0)
-                    spread_panel(1)
-                if j == 1:
-                    spread_panel(2)
-                turn_e(j)
-            if live(jy):
-                turn_y01(jy)
-            if live(jy) or live(jp):
-                pair_rest(turn_rest(jy, jp), jy, jp)
-            if live(jd):
-                shift(jd, 0)
-                weigh(nc.gpsimd, jd, 0)
-                shift(jd, 1)
-                round_y(jd, 0)
-                if j == last:
-                    quant_e(j)
-                shift(jd, 2)
-                weigh(nc.vector, jd, 1)
-                weigh(nc.gpsimd, jd, 2)
-                store_y(jd, slice(0, P))
-            if j != last:
-                quant_e(j)
-                embed(jx, 0)
+            gram(jd, [0, 1, 2])
+            turn_e(j)
+            turn_y01(jy)
+            turn_halves(jy, [jp])
+            finish_y(jd)
+            round_y(jd, 0)
+            quant_e(j)
+            embed(jx, 0)
 
-        round_y(last - 1, 1)
-        round_y(last - 1, 2)
-        gram(last, [0, 1, 2])
-        turn_y01(last - 1)
-        pair_rest(turn_rest(last - 1, -1), last - 1, -1)
+        prev = last - 1
+        scale_e(last, 0)
+        quant_y(last - 3, [0, 1, 2])
+        round_y(last - 2, 1)
+        round_y(last - 2, 2)
+        embed(last, 1)
+        scale_e(last, 1)
+        turn_e(last, [0])
+        gram(prev, [0, 1])
+        turn_e(last, [1])
+        turn_y01(last - 2)
+        turn_halves(last - 2, [])
+        gram(prev, [2])
+        shift(prev, 0)
+        quant_e(last, 0, 1)
+        shift(prev, 1)
+        quant_e(last, 1, 2)
+        for g in range(E_PASSES):
+            for n in range(Y_GROUPS):
+                gram_pass(last, n, g)
+        weigh(nc.vector, prev, 0)
+        store_y(prev, slice(0, BANK))
+        quant_y(last - 2, [0, 1, 2])
+        round_y(prev, 0)
+        shift(prev, 2)
+        weigh(nc.vector, prev, 1)
+        store_y(prev, slice(BANK, 2 * BANK))
+        round_y(prev, 1)
+        weigh(nc.gpsimd, prev, 2)
+        store_y(prev, slice(2 * BANK, P))
+        turn_y01(prev)
+        round_y(prev, 2)
         shift(last, 0)
         shift(last, 1)
-        weigh(nc.gpsimd, last, 0)
         shift(last, 2)
-        for n in range(Y_GROUPS):
-            if n > 0:
-                weigh(nc.vector, last, n)
-            round_y(last, n)
-            store_y(last, slice(n * BANK, (n + 1) * BANK))
-        turn_y01(last)
-        pair_rest(turn_rest(last, -1), last, -1)
-        quant_y(last - 2, [0, 1, 2])
-        quant_y(last - 1, [0, 1, 2])
-        quant_y(last, [0, 1, 2])
-
-        for q in range(4):
-            queue = nc.sync if q % 2 == 0 else nc.scalar
-            queue.dma_start(
-                out=out_2.bitcast(I32)[:, 4 * q:4 * q + 4, :].rearrange("g r w -> r g w"),
-                in_=y_sc[32 * q:32 * q + 4, :, :].bitcast(I32),
-            )
+        weigh(nc.vector, last, 0)
+        round_y(last, 0)
+        store_y(last, slice(0, BANK))
+        weigh(nc.vector, last, 1)
+        round_y(last, 1)
+        store_y(last, slice(BANK, 2 * BANK))
+        weigh_rounded(last, 2)
+        weigh(nc.vector, last, 2)
+        store_y(last, slice(2 * BANK, P))
+        turn_halves(prev, [])
+        turn_y(last, 0)
+        turn_y(last, 2)
+        turn_y(last, 1)
+        quant_y(prev, [0, 1, 2])
+        quant_y(last, [0, 2, 1])

@@ -69,7 +69,6 @@ def tile_community_branch_gram_k6_kernel(
         r_scales = tiles("r_scales", 1, [NP, E_PASSES, P], U8)[0]
 
         ref_sorted = tiles("ref_sorted", 2, [NP, T // 2], F32)
-        pl_sorted = tiles("pl_sorted", 2, [NP, V // 2], F32)
         ref_in = tiles("ref_in", 2, [NP, 2 * BANK], F32)
         ref_codes = tiles("ref_codes", 2, [NP, 4 * NP], U32)
         ref_sc = tiles("ref_sc", 2, [NP, 4 * NP], U8)
@@ -202,8 +201,8 @@ def tile_community_branch_gram_k6_kernel(
 
         def sort_words(engine_copy, dst, src):
             engine_copy(
-                out=dst.rearrange("s (g u p) -> s g u p", u=2, p=NP),
-                in_=src.rearrange("s (g p u) -> s g u p", u=2, p=NP),
+                out=dst.rearrange("s (g u p) -> s g p u", u=2, p=NP),
+                in_=src.rearrange("s (g p u) -> s g p u", u=2, p=NP),
             )
 
         def quantize_inc2(h):
@@ -299,10 +298,10 @@ def tile_community_branch_gram_k6_kernel(
             )
             free.append(g_banks[(j, n)])
 
-        def weigh(engine, j, n):
-            c = slice(n * BANK, (n + 1) * BANK)
+        def weigh(engine, j, n, count=1):
+            c = slice(n * BANK, (n + count) * BANK)
             engine.tensor_tensor(
-                out=y[j % 3][:, c], in0=y[j % 3][:, c], in1=panel_bf[:, P + n * BANK:P + (n + 1) * BANK], op=MULT,
+                out=y[j % 3][:, c], in0=y[j % 3][:, c], in1=panel_bf[:, P + c.start:P + c.stop], op=MULT,
             )
 
         def round_y(j, n, engine_copy=nc.scalar.copy):
@@ -333,10 +332,8 @@ def tile_community_branch_gram_k6_kernel(
                 src = y_bf[Y_GROUPS * (jy % 2) + 2]
                 halves.append((y_in2[jy % 3], [src[:, u * NP:(u + 1) * NP] for u in range(2)]))
             for jp in placed_tiles:
-                if jp < FIRST_SORTED:
+                if live(jp):
                     halves.append((pl_in[jp % 2], [placed[jp][:, u:256:2] for u in range(2)]))
-                elif live(jp):
-                    halves.append((pl_in[jp % 2], [pl_sorted[jp % 2][:, u * NP:(u + 1) * NP] for u in range(2)]))
             for k, (dst, words) in enumerate(halves):
                 for u in range(2):
                     turn(bank, 2 * k + u, words[u])
@@ -385,7 +382,6 @@ def tile_community_branch_gram_k6_kernel(
             free.append(bank)
 
         def sort_tile(j):
-            sort_words(nc.scalar.copy, pl_sorted[j % 2][:], placed[j][:])
             sort_words(nc.scalar.copy, ref_sorted[j % 2][:], ref[j][:])
 
         def interleave_inc(h):
@@ -399,8 +395,7 @@ def tile_community_branch_gram_k6_kernel(
             shift(j, 2)
             if je is not None:
                 quant_e(je)
-            weigh(nc.vector, j, 1)
-            weigh(nc.vector, j, 2)
+            weigh(nc.vector, j, 1, 2)
             store_y(j, slice(0, P))
 
         load_all()

@@ -18,14 +18,23 @@ ADD = mybir.AluOpType.add
 
 NP = 128
 BANK = 512
+PAIRS = BANK // 2
 TILES = S // NP
-REF_PASSES = T // 512
-E_PASSES = B // 512
-Y_GROUPS = P // 512
+LAST = TILES - 1
+REF_PASSES = T // BANK
+E_PASSES = B // BANK
+Y_GROUPS = P // BANK
+ALL_GROUPS = list(range(Y_GROUPS))
+PANEL_ROW = 32
 FIRST_SORTED = 3
 INC_SPLIT = 352
+CODE_RUNS = [(0, 2), (2, 4), (4, 6), (6, 7), (7, 8)]
 SCALE_RUNS = [(0, 6), (6, 8)]
-STORE_RUNS = [(0, 2), (2, 4), (4, 6), (6, 7), (7, 8)]
+
+
+def run_of(runs, j):
+    index = [r for r, (lo, hi) in enumerate(runs) if lo <= j < hi][0]
+    return index, runs[index][0], runs[index][1]
 
 
 def tile_community_branch_gram_k6_kernel(
@@ -51,9 +60,9 @@ def tile_community_branch_gram_k6_kernel(
 
         ident = tiles("ident", 1, [NP, NP], F32)[0]
         rows = tiles("rows", 1, [NP, NP], F32)[0]
-        sw_rows = tiles("sw_rows", 1, [32, NP], BF16)[0]
+        sw_rows = tiles("sw_rows", 1, [PANEL_ROW, NP], BF16)[0]
         root_cols = tiles("root_cols", 1, [NP, 4], F32)[0]
-        cols = tiles("cols", 1, [NP, 64], F32)[0]
+        cols = tiles("cols", 1, [NP, 2 * PANEL_ROW], F32)[0]
         root = tiles("root", 1, [NP, B // 2], F32)[0]
         panel = tiles("panel", 1, [NP, P], F32)[0]
         ref = [None] + tiles("ref", TILES - 1, [NP, T // 2], F32)
@@ -69,23 +78,23 @@ def tile_community_branch_gram_k6_kernel(
         r_scales = tiles("r_scales", 1, [NP, E_PASSES, P], U8)[0]
 
         ref_sorted = tiles("ref_sorted", 2, [NP, T // 2], F32)
-        ref_in = tiles("ref_in", 2, [NP, 2 * BANK], F32)
-        ref_codes = tiles("ref_codes", 2, [NP, 4 * NP], U32)
-        ref_sc = tiles("ref_sc", 2, [NP, 4 * NP], U8)
-        pl_in = tiles("pl_in", 2, [NP, 2 * NP], F32)
+        ref_in = tiles("ref_in", 2, [NP, REF_PASSES * PAIRS], F32)
+        ref_codes = tiles("ref_codes", 2, [NP, REF_PASSES * NP], U32)
+        ref_sc = tiles("ref_sc", 2, [NP, REF_PASSES * NP], U8)
+        pl_in = tiles("pl_in", 2, [NP, PAIRS], F32)
         pl_codes = tiles("pl_codes", 2, [NP, NP], U32)
         pl_sc = tiles("pl_sc", 2, [NP, NP], U8)
-        e_bf = tiles("e_bf", 4, [NP, 2 * NP], F32)
-        e_in = tiles("e_in", 2, [NP, BANK], F32)
-        e_codes = tiles("e_codes", 2, [NP, 2 * NP], U32)
-        e_sc = tiles("e_sc", 2, [NP, 2 * NP], U8)
+        e_bf = tiles("e_bf", 2 * E_PASSES, [NP, PAIRS], F32)
+        e_in = tiles("e_in", 2, [NP, E_PASSES * PAIRS], F32)
+        e_codes = tiles("e_codes", 2, [NP, E_PASSES * NP], U32)
+        e_sc = tiles("e_sc", 2, [NP, E_PASSES * NP], U8)
         y = tiles("y", 3, [NP, P], F32)
-        y_bf = tiles("y_bf", 2 * Y_GROUPS, [NP, 2 * NP], F32)
-        y_in01 = tiles("y_in01", 3, [NP, BANK], F32)
-        y_in2 = tiles("y_in2", 3, [NP, 2 * NP], F32)
+        y_bf = tiles("y_bf", 2 * Y_GROUPS, [NP, PAIRS], F32)
+        y_in01 = tiles("y_in01", 3, [NP, 2 * PAIRS], F32)
+        y_in2 = tiles("y_in2", 3, [NP, PAIRS], F32)
         y_codes = [
             sb.tile([NP, Y_GROUPS, (hi - lo) * NP], U32, name="y_codes%d" % lo, align_bytes=64)
-            for lo, hi in STORE_RUNS
+            for lo, hi in CODE_RUNS
         ]
         y_sc = [
             sb.tile([NP, Y_GROUPS, (hi - lo) * NP], U8, name="y_sc%d" % lo, align_bytes=64) for lo, hi in SCALE_RUNS
@@ -97,21 +106,20 @@ def tile_community_branch_gram_k6_kernel(
         nc.vector.memset(r_scales[:].rearrange("p g n -> p (g n)").bitcast(I32), 0)
         make_identity(nc, ident[:])
 
-        ref_w = ref_dev.bitcast(F32)
-        placed_w = placed_dev.bitcast(F32)
-        inc_k = placed_inc.rearrange("(p j) n -> p j n", j=4)
+        ref_pairs = ref_dev.bitcast(F32)
+        placed_pairs = placed_dev.bitcast(F32)
         w_words = ref_words.bitcast(I32)
         r_words = panel_words.rearrange("g p n t -> p g (n t)").bitcast(I32)
 
-        def load_ref(i):
-            nc.sync.dma_start(out=ref[i][:], in_=ref_w[i * NP:(i + 1) * NP, :])
+        def load_ref(j):
+            nc.sync.dma_start(out=ref[j][:], in_=ref_pairs[j * NP:(j + 1) * NP, :])
 
-        def load_placed(i):
-            nc.sync.dma_start(out=placed[i][:], in_=placed_w[i * NP:(i + 1) * NP, :])
+        def load_placed(j):
+            nc.sync.dma_start(out=placed[j][:], in_=placed_pairs[j * NP:(j + 1) * NP, :])
 
-        def load_w(h):
-            src = w_words[2 * h:2 * h + 2, :, :].rearrange("g p w -> p g w")
-            nc.sync.dma_start(out=w_codes[h][:].bitcast(I32), in_=src)
+        def load_w(half):
+            src = w_words[2 * half:2 * half + 2, :, :].rearrange("g p w -> p g w")
+            nc.sync.dma_start(out=w_codes[half][:].bitcast(I32), in_=src)
 
         def load_scales(plane, src, passes):
             for q in range(4):
@@ -120,35 +128,35 @@ def tile_community_branch_gram_k6_kernel(
                     in_=src.bitcast(I32)[passes, 4 * q:4 * q + 4, :].rearrange("g r w -> r g w"),
                 )
 
-        def word_rows(vec):
-            return vec.rearrange("(m w) -> m w", w=2 * NP).bitcast(F32)
+        def load_pair_rows(first_row, vec):
+            src = vec.rearrange("(m w) -> m w", w=2 * NP).bitcast(F32)
+            nc.gpsimd.dma_start(out=rows[first_row:first_row + src.shape[0], :], in_=src)
 
-        def load_all():
-            for half in range(2):
-                nc.sync.dma_start(out=ref_first[half][:], in_=ref_w[0:NP, half * BANK:(half + 1) * BANK])
-            nc.sync.dma_start(out=root_cols[:], in_=root_length.rearrange("(p w) -> p w", p=NP).bitcast(F32))
-            nc.gpsimd.dma_start(out=sw_rows[0:TILES, :], in_=sample_weight.rearrange("(i p) -> i p", p=NP))
-            nc.gpsimd.dma_start(out=rows[32:38, :], in_=word_rows(offset))
-            nc.gpsimd.dma_start(out=rows[38:44, :], in_=word_rows(panel_weight))
-            load_scales(w_scales, ref_scales, slice(0, 2))
-            load_w(0)
-            load_ref(1)
-            load_scales(w_scales, ref_scales, slice(2, 4))
-            load_w(1)
-            load_placed(0)
-            load_placed(1)
-            nc.sync.dma_start(out=inc_raw[:], in_=inc_k)
-            load_ref(2)
-            load_placed(2)
-            load_scales(r_scales, panel_scales, slice(0, 2))
-            for n in range(Y_GROUPS):
-                nc.sync.dma_start(out=r_codes[n][:].bitcast(I32), in_=r_words[:, :, n * BANK:(n + 1) * BANK])
-            for i in range(3, TILES):
-                load_ref(i)
-                load_placed(i)
+        for half in range(2):
+            nc.sync.dma_start(out=ref_first[half][:], in_=ref_pairs[0:NP, half * BANK:(half + 1) * BANK])
+        nc.sync.dma_start(out=root_cols[:], in_=root_length.rearrange("(p w) -> p w", p=NP).bitcast(F32))
+        nc.gpsimd.dma_start(out=sw_rows[0:TILES, :], in_=sample_weight.rearrange("(i p) -> i p", p=NP))
+        load_pair_rows(PANEL_ROW, offset)
+        load_pair_rows(PANEL_ROW + P // (2 * NP), panel_weight)
+        load_scales(w_scales, ref_scales, slice(0, 2))
+        load_w(0)
+        load_ref(1)
+        load_scales(w_scales, ref_scales, slice(2, 4))
+        load_w(1)
+        load_placed(0)
+        load_placed(1)
+        nc.sync.dma_start(out=inc_raw[:], in_=placed_inc.rearrange("(p t) n -> p t n", t=4))
+        load_ref(2)
+        load_placed(2)
+        load_scales(r_scales, panel_scales, slice(0, E_PASSES))
+        for n in ALL_GROUPS:
+            nc.sync.dma_start(out=r_codes[n][:].bitcast(I32), in_=r_words[:, :, n * BANK:(n + 1) * BANK])
+        for j in range(3, TILES):
+            load_ref(j)
+            load_placed(j)
 
-        def live(i):
-            return 0 <= i < TILES
+        def live(j):
+            return 0 <= j < TILES
 
         def turn(bank, slot, words):
             nc.tensor.transpose(banks[bank][:, slot * NP:(slot + 1) * NP], words, ident[:])
@@ -162,11 +170,11 @@ def tile_community_branch_gram_k6_kernel(
         def quantize(codes, scales, src):
             nc.vector.quantize_mx(out=codes.bitcast(FP8X4), scales=scales, in_=src.bitcast(BF16))
 
-        def sorted_read(ap):
+        def sorting_view(ap):
             return ap.rearrange("s (p u e) -> s u p e", u=2, e=2)
 
-        def sorted_write(ap):
-            return ap.bitcast(BF16).rearrange("s (u p e) -> s u p e", u=2, e=2)
+        def sorted_view(ap):
+            return ap.rearrange("s (u p e) -> s u p e", u=2, e=2)
 
         def spread(bank, src, first):
             for m in range(4):
@@ -175,7 +183,7 @@ def tile_community_branch_gram_k6_kernel(
         def turn_vectors():
             bank = take_bank()
             turn(bank, 0, rows[:])
-            nc.scalar.copy(out=cols[:], in_=banks[bank][:, 0:64])
+            nc.scalar.copy(out=cols[:], in_=banks[bank][:, 0:2 * PANEL_ROW])
             free.append(bank)
 
         def spread_root():
@@ -187,51 +195,55 @@ def tile_community_branch_gram_k6_kernel(
             )
             free.append(bank)
 
-        def spread_panel(k):
+        def spread_panel(third):
             bank = take_bank()
-            spread(bank, cols, 32 + 4 * k)
-            nc.scalar.copy(out=panel[:, k * BANK:(k + 1) * BANK], in_=banks[bank][:])
+            spread(bank, cols, PANEL_ROW + 4 * third)
+            nc.scalar.copy(out=panel[:, third * BANK:(third + 1) * BANK], in_=banks[bank][:])
             free.append(bank)
 
-        def quantize_inc(h, engine_copy, lo, hi):
-            engine_copy(
-                out=inc_in[h][:, 4 * lo:4 * hi].rearrange("p (c i t) -> p c t i", i=4, t=4),
-                in_=inc_raw[:, :, h * BANK + lo:h * BANK + hi].rearrange("p t (c i) -> p c t i", i=4),
-            )
+        def interleave_inc(h):
+            for engine_copy, lo, hi in ((nc.vector.tensor_copy, 0, INC_SPLIT), (nc.scalar.copy, INC_SPLIT, BANK)):
+                engine_copy(
+                    out=inc_in[h][:, 4 * lo:4 * hi].rearrange("p (c i t) -> p c t i", i=4, t=4),
+                    in_=inc_raw[:, :, h * BANK + lo:h * BANK + hi].rearrange("p t (c i) -> p c t i", i=4),
+                )
 
-        def sort_words(engine_copy, dst, src):
-            engine_copy(
-                out=dst.rearrange("s (g u p) -> s g p u", u=2, p=NP),
-                in_=src.rearrange("s (g p u) -> s g p u", u=2, p=NP),
-            )
-
-        def quantize_inc2(h):
+        def quant_inc(h):
             nc.vector.quantize_mx(out=inc_codes[h][:].bitcast(FP8X4), scales=inc_scales[h][:], in_=inc_in[h][:])
 
-        panel_bf = panel[:].bitcast(BF16)
-        root_bf = root[:].bitcast(BF16)
-        e_banks = {}
-        g_banks = {}
+        def sort_ref(j):
+            nc.scalar.copy(
+                out=ref_sorted[j % 2][:].rearrange("s (g u p) -> s g p u", u=2, p=NP),
+                in_=ref[j][:].rearrange("s (g p u) -> s g p u", u=2, p=NP),
+            )
 
         def turn_ref(j):
             for half in range(2):
                 bank = take_bank()
                 for g in range(2):
                     for u in range(2):
-                        k0 = 256 * (2 * half + g)
+                        first = PAIRS * (2 * half + g)
                         if j == 0:
-                            words = ref_first[half][:, 256 * g + u:256 * (g + 1):2]
+                            words = ref_first[half][:, PAIRS * g + u:PAIRS * (g + 1):2]
                         elif j < FIRST_SORTED:
-                            words = ref[j][:, k0 + u:k0 + 256:2]
+                            words = ref[j][:, first + u:first + PAIRS:2]
                         else:
-                            words = ref_sorted[j % 2][:, k0 + u * NP:k0 + (u + 1) * NP]
+                            words = ref_sorted[j % 2][:, first + u * NP:first + (u + 1) * NP]
                         turn(bank, 2 * g + u, words)
                 pair_up(ref_in[j % 2][:, half * BANK:(half + 1) * BANK], banks[bank][:])
                 free.append(bank)
 
         def quant_ref(j, lo, hi):
             c = slice(lo * NP, hi * NP)
-            quantize(ref_codes[j % 2][:, c], ref_sc[j % 2][:, c], ref_in[j % 2][:, lo * 256:hi * 256])
+            quantize(ref_codes[j % 2][:, c], ref_sc[j % 2][:, c], ref_in[j % 2][:, lo * PAIRS:hi * PAIRS])
+
+        def quant_placed(j):
+            quantize(pl_codes[j % 2][:], pl_sc[j % 2][:], pl_in[j % 2][:])
+
+        panel_bf = panel[:].bitcast(BF16)
+        root_bf = root[:].bitcast(BF16)
+        e_banks = {}
+        g_banks = {}
 
         def embed_ref(j, h, passes):
             for g in passes:
@@ -259,36 +271,35 @@ def tile_community_branch_gram_k6_kernel(
 
         def scale_e(j, h):
             nc.vector.tensor_tensor(
-                out=sorted_write(e_bf[2 * (j % 2) + h][:]),
-                in0=sorted_read(banks[e_banks[(j, h)]][:]),
-                in1=root_bf[:, h * BANK:(h + 1) * BANK].rearrange("s (u p e) -> s u p e", u=2, e=2),
+                out=sorted_view(e_bf[E_PASSES * (j % 2) + h][:].bitcast(BF16)),
+                in0=sorting_view(banks[e_banks[(j, h)]][:]),
+                in1=sorted_view(root_bf[:, h * BANK:(h + 1) * BANK]),
                 op=MULT,
             )
             free.append(e_banks[(j, h)])
 
-        def turn_e(j, passes=(0, 1)):
+        def turn_e(j):
             bank = take_bank()
-            for g in passes:
+            for g in range(E_PASSES):
                 for u in range(2):
-                    turn(bank, 2 * g + u, e_bf[2 * (j % 2) + g][:, u * NP:(u + 1) * NP])
-            c = slice(passes[0] * 256, (passes[-1] + 1) * 256)
-            pair_up(e_in[j % 2][:, c], banks[bank][:, c])
+                    turn(bank, 2 * g + u, e_bf[E_PASSES * (j % 2) + g][:, u * NP:(u + 1) * NP])
+            pair_up(e_in[j % 2][:], banks[bank][:])
             free.append(bank)
 
-        def gram_pass(j, n, g):
-            if g == 0:
-                g_banks[(j, n)] = take_bank()
-            c = slice(g * NP, (g + 1) * NP)
-            nc.tensor.matmul_mx(
-                out=banks[g_banks[(j, n)]][:], lhsT=e_codes[j % 2][:, c].bitcast(FP8X4), lhsT_scale=e_sc[j % 2][:, c],
-                rhs=r_codes[n][:, g, :].bitcast(FP8X4), rhs_scale=r_scales[:, g, n * BANK:(n + 1) * BANK],
-                start=(g == 0), stop=(g == E_PASSES - 1),
-            )
+        def quant_e(j):
+            quantize(e_codes[j % 2][:], e_sc[j % 2][:], e_in[j % 2][:])
 
         def gram(j, groups):
             for n in groups:
+                g_banks[(j, n)] = take_bank()
                 for g in range(E_PASSES):
-                    gram_pass(j, n, g)
+                    c = slice(g * NP, (g + 1) * NP)
+                    nc.tensor.matmul_mx(
+                        out=banks[g_banks[(j, n)]][:],
+                        lhsT=e_codes[j % 2][:, c].bitcast(FP8X4), lhsT_scale=e_sc[j % 2][:, c],
+                        rhs=r_codes[n][:, g, :].bitcast(FP8X4), rhs_scale=r_scales[:, g, n * BANK:(n + 1) * BANK],
+                        start=(g == 0), stop=(g == E_PASSES - 1),
+                    )
 
         def shift(j, n):
             c = slice(n * BANK, (n + 1) * BANK)
@@ -304,131 +315,109 @@ def tile_community_branch_gram_k6_kernel(
                 out=y[j % 3][:, c], in0=y[j % 3][:, c], in1=panel_bf[:, P + c.start:P + c.stop], op=MULT,
             )
 
-        def round_y(j, n, engine_copy=nc.scalar.copy):
-            engine_copy(
-                out=sorted_write(y_bf[Y_GROUPS * (j % 2) + n][:]),
-                in_=sorted_read(y[j % 3][:, n * BANK:(n + 1) * BANK]),
+        def round_y(j, n):
+            nc.scalar.copy(
+                out=sorted_view(y_bf[Y_GROUPS * (j % 2) + n][:].bitcast(BF16)),
+                in_=sorting_view(y[j % 3][:, n * BANK:(n + 1) * BANK]),
             )
 
         def weigh_rounded(j, n):
             c = slice(n * BANK, (n + 1) * BANK)
             nc.vector.tensor_tensor(
-                out=sorted_write(y_bf[Y_GROUPS * (j % 2) + n][:]), in0=sorted_read(y[j % 3][:, c]),
-                in1=sorted_read(panel_bf[:, P + n * BANK:P + (n + 1) * BANK]), op=MULT,
+                out=sorted_view(y_bf[Y_GROUPS * (j % 2) + n][:].bitcast(BF16)), in0=sorting_view(y[j % 3][:, c]),
+                in1=sorting_view(panel_bf[:, P + c.start:P + c.stop]), op=MULT,
             )
+
+        def store_y(j, n, count=1):
+            c = slice(n * BANK, (n + count) * BANK)
+            nc.sync.dma_start(out=out_0[j * NP:(j + 1) * NP, c], in_=y[j % 3][:, c])
+
+        def y_words(j, n):
+            src = y_bf[Y_GROUPS * (j % 2) + n]
+            return [src[:, u * NP:(u + 1) * NP] for u in range(2)]
+
+        def y_in(j, n):
+            return y_in01[j % 3][:, n * PAIRS:(n + 1) * PAIRS] if n < 2 else y_in2[j % 3][:]
 
         def turn_y01(j):
             bank = take_bank()
-            for g in range(2):
+            for n in range(2):
                 for u in range(2):
-                    turn(bank, 2 * g + u, y_bf[Y_GROUPS * (j % 2) + g][:, u * NP:(u + 1) * NP])
+                    turn(bank, 2 * n + u, y_words(j, n)[u])
             pair_up(y_in01[j % 3][:], banks[bank][:])
             free.append(bank)
 
-        def turn_halves(jy, placed_tiles):
+        def turn_halves(y_groups, placed_tiles):
             bank = take_bank()
-            halves = []
-            if live(jy):
-                src = y_bf[Y_GROUPS * (jy % 2) + 2]
-                halves.append((y_in2[jy % 3], [src[:, u * NP:(u + 1) * NP] for u in range(2)]))
-            for jp in placed_tiles:
-                if live(jp):
-                    halves.append((pl_in[jp % 2], [placed[jp][:, u:256:2] for u in range(2)]))
+            halves = [(y_in(j, n), y_words(j, n)) for j, n in y_groups]
+            for j in placed_tiles:
+                halves.append((pl_in[j % 2][:], [placed[j][:, u:PAIRS:2] for u in range(2)]))
             for k, (dst, words) in enumerate(halves):
                 for u in range(2):
                     turn(bank, 2 * k + u, words[u])
             for k, (dst, words) in enumerate(halves):
-                pair_up(dst[:], banks[bank][:, k * 256:(k + 1) * 256])
+                pair_up(dst, banks[bank][:, k * PAIRS:(k + 1) * PAIRS])
             free.append(bank)
 
         def quant_y(j, groups):
-            run = [r for r, (lo, hi) in enumerate(STORE_RUNS) if lo <= j < hi][0]
-            lo, hi = STORE_RUNS[run]
-            srun = [r for r, (slo, shi) in enumerate(SCALE_RUNS) if slo <= j < shi][0]
-            slo, shi = SCALE_RUNS[srun]
-            for g in groups:
-                src = y_in01[j % 3][:, g * 256:(g + 1) * 256] if g < 2 else y_in2[j % 3][:]
+            run, lo, hi = run_of(CODE_RUNS, j)
+            sc_run, sc_lo, sc_hi = run_of(SCALE_RUNS, j)
+            for n in groups:
                 quantize(
-                    y_codes[run][:, g, (j - lo) * NP:(j - lo + 1) * NP],
-                    y_sc[srun][:, g, (j - slo) * NP:(j - slo + 1) * NP], src,
+                    y_codes[run][:, n, (j - lo) * NP:(j - lo + 1) * NP],
+                    y_sc[sc_run][:, n, (j - sc_lo) * NP:(j - sc_lo + 1) * NP], y_in(j, n),
                 )
             if j == hi - 1:
                 dst = out_1.rearrange("g p m t -> p g (m t)").bitcast(I32)[:, :, lo * NP:hi * NP]
                 nc.sync.dma_start(out=dst, in_=y_codes[run][:].bitcast(I32))
-            if j == shi - 1:
+            if j == sc_hi - 1:
                 for q in range(4):
-                    queue = nc.scalar if j == TILES - 1 and q % 2 == 1 else nc.sync
-                    dst = out_2.bitcast(I32)[:, 4 * q:4 * q + 4, slo * NP // 4:shi * NP // 4]
+                    queue = nc.scalar if j == LAST and q % 2 == 1 else nc.sync
+                    dst = out_2.bitcast(I32)[:, 4 * q:4 * q + 4, sc_lo * NP // 4:sc_hi * NP // 4]
                     queue.dma_start(
-                        out=dst.rearrange("g r w -> r g w"), in_=y_sc[srun][32 * q:32 * q + 4, :, :].bitcast(I32),
+                        out=dst.rearrange("g r w -> r g w"), in_=y_sc[sc_run][32 * q:32 * q + 4, :, :].bitcast(I32),
                     )
 
-        def store_y(j, c):
-            nc.sync.dma_start(out=out_0[j * NP:(j + 1) * NP, c], in_=y[j % 3][:, c])
-
-        def quant_placed(j):
-            quantize(pl_codes[j % 2][:], pl_sc[j % 2][:], pl_in[j % 2][:])
-
-        def quant_e(j, lo=0, hi=2):
-            c = slice(lo * NP, hi * NP)
-            quantize(e_codes[j % 2][:, c], e_sc[j % 2][:, c], e_in[j % 2][:, lo * 256:hi * 256])
-
-        def turn_y(j, n):
-            bank = take_bank()
-            for u in range(2):
-                turn(bank, u, y_bf[Y_GROUPS * (j % 2) + n][:, u * NP:(u + 1) * NP])
-            dst = y_in01[j % 3][:, n * 256:(n + 1) * 256] if n < 2 else y_in2[j % 3][:]
-            pair_up(dst, banks[bank][:, 0:256])
-            free.append(bank)
-
-        def sort_tile(j):
-            sort_words(nc.scalar.copy, ref_sorted[j % 2][:], ref[j][:])
-
-        def interleave_inc(h):
-            quantize_inc(h, nc.vector.tensor_copy, 0, INC_SPLIT)
-            quantize_inc(h, nc.scalar.copy, INC_SPLIT, BANK)
-
-        def finish_y(j, je=None):
+        def shift_all(j):
             shift(j, 0)
             weigh(nc.gpsimd, j, 0)
             shift(j, 1)
             shift(j, 2)
-            if je is not None:
-                quant_e(je)
-            weigh(nc.vector, j, 1, 2)
-            store_y(j, slice(0, P))
 
-        load_all()
+        def weigh_rest(j):
+            weigh(nc.vector, j, 1, Y_GROUPS - 1)
+            store_y(j, 0, Y_GROUPS)
+
         turn_ref(0)
         spread_root()
         quant_ref(0, 0, 2)
         quant_ref(0, 2, 4)
-        nc.vector.tensor_copy(out=rows[0:32, :], in_=sw_rows[:])
-        embed_ref(0, 0, [0, 1])
-        embed_ref(0, 1, [0, 1])
+        nc.vector.tensor_copy(out=rows[0:PANEL_ROW, :], in_=sw_rows[:])
+        for h in range(E_PASSES):
+            embed_ref(0, h, [0, 1])
         turn_ref(1)
         quant_ref(1, 0, 2)
         quant_ref(1, 2, 4)
-        embed_ref(0, 0, [2, 3])
-        embed_ref(0, 1, [2, 3])
-        interleave_inc(0)
-        interleave_inc(1)
-        turn_halves(-1, [0, 1])
+        for h in range(E_PASSES):
+            embed_ref(0, h, [2, 3])
+        for h in range(E_PASSES):
+            interleave_inc(h)
+        turn_halves([], [0, 1])
         turn_vectors()
-        quantize_inc2(0)
+        quant_inc(0)
         quant_placed(0)
-        quantize_inc2(1)
+        quant_inc(1)
         quant_placed(1)
-        embed_ref(1, 0, range(REF_PASSES))
+        for h in range(E_PASSES):
+            embed_ref(1, h, range(REF_PASSES))
         turn_ref(2)
-        turn_halves(-1, [2])
-        embed_ref(1, 1, range(REF_PASSES))
+        turn_halves([], [2])
         for j in range(2):
             for h in range(E_PASSES):
                 embed_placed(j, h)
-        quant_ref(2, 0, 4)
         scale_e(0, 0)
         scale_e(0, 1)
+        quant_ref(2, 0, REF_PASSES)
         quant_placed(2)
         spread_panel(0)
         turn_e(0)
@@ -438,87 +427,83 @@ def tile_community_branch_gram_k6_kernel(
         quant_e(0)
         scale_e(1, 1)
         embed(2, 0)
-        gram(0, [0, 1, 2])
-        sort_tile(3)
+        gram(0, ALL_GROUPS)
+        sort_ref(3)
         scale_e(2, 0)
         turn_e(1)
-        finish_y(0, 1)
+        shift_all(0)
+        quant_e(1)
+        weigh_rest(0)
+        turn_ref(3)
+        turn_halves([], [3])
+        for n in ALL_GROUPS:
+            round_y(0, n)
+        sort_ref(4)
+        quant_placed(3)
+        quant_ref(3, 0, REF_PASSES)
+        embed(2, 1)
+        scale_e(2, 1)
+        gram(1, ALL_GROUPS)
 
-        last = TILES - 1
-        for j in range(2, last):
-            jx, jd, jy, jp = j + 1, j - 1, j - 2, j + 2
-            if j > 2:
-                scale_e(j, 0)
-            if live(j - 3):
-                quant_y(j - 3, [0, 1, 2])
-            turn_ref(jx)
-            if j == 2:
-                turn_halves(-1, [jx])
-                round_y(0, 0)
-            round_y(jy, 1)
-            round_y(jy, 2)
-            if live(jp):
-                sort_tile(jp)
-            quant_placed(jx)
-            quant_ref(jx, 0, 4)
+        for j in range(3, TILES):
+            j_in, j_e, j_g, j_y = j + 1, j - 1, j - 2, j - 3
+            turn_e(j_e)
+            turn_y01(j_y)
+            turn_halves([(j_y, 2)], [j_in] if live(j_in) else [])
+            shift_all(j_g)
+            weigh_rest(j_g)
+            if live(j_in):
+                turn_ref(j_in)
+            for n in ALL_GROUPS:
+                round_y(j_g, n)
+            if live(j_in + 1):
+                sort_ref(j_in + 1)
+            quant_e(j_e)
+            quant_y(j_y, ALL_GROUPS)
+            embed(j, 0)
+            scale_e(j, 0)
+            if live(j_in):
+                quant_placed(j_in)
+                quant_ref(j_in, 0, REF_PASSES)
             embed(j, 1)
             scale_e(j, 1)
-            gram(jd, [0, 1, 2])
-            turn_e(j)
-            turn_y01(jy)
-            turn_halves(jy, [jp])
-            finish_y(jd)
-            round_y(jd, 0)
-            quant_e(j)
-            embed(jx, 0)
+            if j < LAST:
+                gram(j_e, ALL_GROUPS)
 
-        prev = last - 1
-        scale_e(last, 0)
-        quant_y(last - 3, [0, 1, 2])
-        round_y(last - 2, 1)
-        round_y(last - 2, 2)
-        embed(last, 1)
-        scale_e(last, 1)
-        turn_e(last, [0])
+        prev = LAST - 1
         gram(prev, [0, 1])
-        turn_e(last, [1])
-        turn_y01(last - 2)
-        turn_halves(last - 2, [])
+        turn_e(LAST)
+        turn_y01(prev - 1)
+        turn_halves([(prev - 1, 2)], [])
         gram(prev, [2])
         shift(prev, 0)
-        quant_e(last, 0, 1)
         shift(prev, 1)
-        quant_e(last, 1, 2)
-        for g in range(E_PASSES):
-            for n in range(Y_GROUPS):
-                gram_pass(last, n, g)
         weigh(nc.vector, prev, 0)
-        store_y(prev, slice(0, BANK))
-        quant_y(last - 2, [0, 1, 2])
+        quant_e(LAST)
+        gram(LAST, ALL_GROUPS)
+        store_y(prev, 0)
+        quant_y(prev - 1, ALL_GROUPS)
         round_y(prev, 0)
         shift(prev, 2)
         weigh(nc.vector, prev, 1)
-        store_y(prev, slice(BANK, 2 * BANK))
+        store_y(prev, 1)
         round_y(prev, 1)
         weigh(nc.gpsimd, prev, 2)
-        store_y(prev, slice(2 * BANK, P))
+        store_y(prev, 2)
         turn_y01(prev)
         round_y(prev, 2)
-        shift(last, 0)
-        shift(last, 1)
-        shift(last, 2)
-        weigh(nc.vector, last, 0)
-        round_y(last, 0)
-        store_y(last, slice(0, BANK))
-        weigh(nc.vector, last, 1)
-        round_y(last, 1)
-        store_y(last, slice(BANK, 2 * BANK))
-        weigh_rounded(last, 2)
-        weigh(nc.vector, last, 2)
-        store_y(last, slice(2 * BANK, P))
-        turn_halves(prev, [])
-        turn_y(last, 0)
-        turn_y(last, 2)
-        turn_y(last, 1)
-        quant_y(prev, [0, 1, 2])
-        quant_y(last, [0, 2, 1])
+        for n in ALL_GROUPS:
+            shift(LAST, n)
+        for n in range(2):
+            weigh(nc.vector, LAST, n)
+            round_y(LAST, n)
+            store_y(LAST, n)
+        weigh_rounded(LAST, 2)
+        weigh(nc.vector, LAST, 2)
+        store_y(LAST, 2)
+        turn_halves([(prev, 2)], [])
+        ready_order = [0, 2, 1]
+        for n in ready_order:
+            turn_halves([(LAST, n)], [])
+        quant_y(prev, ALL_GROUPS)
+        quant_y(LAST, ready_order)

from contextlib import ExitStack

import concourse.mybir as mybir
from concourse.masks import make_identity

S, T, V, B, P = 1024, 2048, 512, 1024, 1536
FLOPS = 2 * S * (T + V) * B + 2 * S * B * P

F32 = mybir.dt.float32
BF16 = mybir.dt.bfloat16
I32 = mybir.dt.int32
U32 = mybir.dt.uint32
U8 = mybir.dt.uint8
FP8X4 = mybir.dt.float8_e4m3fn_x4
FP4X4 = mybir.dt.float4_e2m1fn_x4
MULT = mybir.AluOpType.mult
ADD = mybir.AluOpType.add

NP = 128
BANK = 512
PAIRS = BANK // 2
TILES = S // NP
LAST = TILES - 1
REF_PASSES = T // BANK
E_PASSES = B // BANK
Y_GROUPS = P // BANK
ALL_GROUPS = list(range(Y_GROUPS))
PANEL_ROW = 32
FIRST_SORTED = 3
INC_SPLIT = 352
CODE_RUNS = [(0, 2), (2, 4), (4, 6), (6, 7), (7, 8)]
SCALE_RUNS = [(0, 6), (6, 8)]


def run_of(runs, j):
    index = [r for r, (lo, hi) in enumerate(runs) if lo <= j < hi][0]
    return index, runs[index][0], runs[index][1]


def tile_community_branch_gram_k6_kernel(
    tc, ref_dev, placed_dev, ref_words, ref_scales, placed_inc, root_length,
    panel_words, panel_scales, sample_weight, offset, panel_weight, out_0, out_1, out_2,
):
    nc = tc.nc
    with ExitStack() as ctx:
        sb = ctx.enter_context(tc.tile_pool(name="sb", bufs=1))
        ps = ctx.enter_context(tc.psum_pool(name="ps", bufs=1))
        ctx.enter_context(tc.manual_schedule())

        def tiles(name, count, shape, dtype):
            return [sb.tile(shape, dtype, name="%s%d" % (name, i), align_bytes=64) for i in range(count)]

        banks = [ps.tile([NP, BANK], F32, name="bank%d" % i) for i in range(8)]
        free = list(range(len(banks)))

        def take_bank():
            index = free[0]
            free.remove(index)
            return index

        ident = tiles("ident", 1, [NP, NP], F32)[0]
        rows = tiles("rows", 1, [NP, NP], F32)[0]
        sw_rows = tiles("sw_rows", 1, [PANEL_ROW, NP], BF16)[0]
        root_cols = tiles("root_cols", 1, [NP, 4], F32)[0]
        cols = tiles("cols", 1, [NP, 2 * PANEL_ROW], F32)[0]
        root = tiles("root", 1, [NP, B // 2], F32)[0]
        panel = tiles("panel", 1, [NP, P], F32)[0]
        ref = [None] + tiles("ref", TILES - 1, [NP, T // 2], F32)
        ref_first = tiles("ref_first", 2, [NP, T // 4], F32)
        placed = tiles("placed", TILES, [NP, V // 2], F32)
        w_codes = tiles("w_codes", REF_PASSES // 2, [NP, 2, 2 * B], U8)
        w_scales = tiles("w_scales", 1, [NP, REF_PASSES, B], U8)[0]
        inc_raw = tiles("inc_raw", 1, [NP, 4, B], BF16)[0]
        inc_in = tiles("inc_in", E_PASSES, [NP, 4 * BANK], BF16)
        inc_codes = tiles("inc_codes", E_PASSES, [NP, BANK], U32)
        inc_scales = tiles("inc_scales", E_PASSES, [NP, BANK], U8)
        r_codes = tiles("r_codes", Y_GROUPS, [NP, E_PASSES, BANK], U32)
        r_scales = tiles("r_scales", 1, [NP, E_PASSES, P], U8)[0]

        ref_sorted = tiles("ref_sorted", 2, [NP, T // 2], F32)
        ref_in = tiles("ref_in", 2, [NP, REF_PASSES * PAIRS], F32)
        ref_codes = tiles("ref_codes", 2, [NP, REF_PASSES * NP], U32)
        ref_sc = tiles("ref_sc", 2, [NP, REF_PASSES * NP], U8)
        pl_in = tiles("pl_in", 2, [NP, PAIRS], F32)
        pl_codes = tiles("pl_codes", 2, [NP, NP], U32)
        pl_sc = tiles("pl_sc", 2, [NP, NP], U8)
        e_bf = tiles("e_bf", 2 * E_PASSES, [NP, PAIRS], F32)
        e_in = tiles("e_in", 2, [NP, E_PASSES * PAIRS], F32)
        e_codes = tiles("e_codes", 2, [NP, E_PASSES * NP], U32)
        e_sc = tiles("e_sc", 2, [NP, E_PASSES * NP], U8)
        y = tiles("y", 3, [NP, P], F32)
        y_bf = tiles("y_bf", 2 * Y_GROUPS, [NP, PAIRS], F32)
        y_in01 = tiles("y_in01", 3, [NP, 2 * PAIRS], F32)
        y_in2 = tiles("y_in2", 3, [NP, PAIRS], F32)
        y_codes = [
            sb.tile([NP, Y_GROUPS, (hi - lo) * NP], U32, name="y_codes%d" % lo, align_bytes=64)
            for lo, hi in CODE_RUNS
        ]
        y_sc = [
            sb.tile([NP, Y_GROUPS, (hi - lo) * NP], U8, name="y_sc%d" % lo, align_bytes=64) for lo, hi in SCALE_RUNS
        ]

        nc.vector.memset(w_scales[:].rearrange("p g n -> p (g n)").bitcast(I32), 0)
        nc.vector.memset(rows[:], 0.0)
        nc.vector.memset(sw_rows[:], 0.0)
        nc.vector.memset(r_scales[:].rearrange("p g n -> p (g n)").bitcast(I32), 0)
        make_identity(nc, ident[:])

        ref_pairs = ref_dev.bitcast(F32)
        placed_pairs = placed_dev.bitcast(F32)
        w_words = ref_words.bitcast(I32)
        r_words = panel_words.rearrange("g p n t -> p g (n t)").bitcast(I32)

        def load_ref(j):
            nc.sync.dma_start(out=ref[j][:], in_=ref_pairs[j * NP:(j + 1) * NP, :])

        def load_placed(j):
            nc.sync.dma_start(out=placed[j][:], in_=placed_pairs[j * NP:(j + 1) * NP, :])

        def load_w(half):
            src = w_words[2 * half:2 * half + 2, :, :].rearrange("g p w -> p g w")
            nc.sync.dma_start(out=w_codes[half][:].bitcast(I32), in_=src)

        def load_scales(plane, src, passes):
            for q in range(4):
                nc.sync.dma_start(
                    out=plane[32 * q:32 * q + 4, passes, :].bitcast(I32),
                    in_=src.bitcast(I32)[passes, 4 * q:4 * q + 4, :].rearrange("g r w -> r g w"),
                )

        def load_pair_rows(first_row, vec):
            src = vec.rearrange("(m w) -> m w", w=2 * NP).bitcast(F32)
            nc.gpsimd.dma_start(out=rows[first_row:first_row + src.shape[0], :], in_=src)

        for half in range(2):
            nc.sync.dma_start(out=ref_first[half][:], in_=ref_pairs[0:NP, half * BANK:(half + 1) * BANK])
        nc.sync.dma_start(out=root_cols[:], in_=root_length.rearrange("(p w) -> p w", p=NP).bitcast(F32))
        nc.gpsimd.dma_start(out=sw_rows[0:TILES, :], in_=sample_weight.rearrange("(i p) -> i p", p=NP))
        load_pair_rows(PANEL_ROW, offset)
        load_pair_rows(PANEL_ROW + P // (2 * NP), panel_weight)
        load_scales(w_scales, ref_scales, slice(0, 2))
        load_w(0)
        load_ref(1)
        load_scales(w_scales, ref_scales, slice(2, 4))
        load_w(1)
        load_placed(0)
        load_placed(1)
        nc.sync.dma_start(out=inc_raw[:], in_=placed_inc.rearrange("(p t) n -> p t n", t=4))
        load_ref(2)
        load_placed(2)
        load_scales(r_scales, panel_scales, slice(0, E_PASSES))
        for n in ALL_GROUPS:
            nc.sync.dma_start(out=r_codes[n][:].bitcast(I32), in_=r_words[:, :, n * BANK:(n + 1) * BANK])
        for j in range(3, TILES):
            load_ref(j)
            load_placed(j)

        def live(j):
            return 0 <= j < TILES

        def turn(bank, slot, words):
            nc.tensor.transpose(banks[bank][:, slot * NP:(slot + 1) * NP], words, ident[:])

        def pair_up(dst, src):
            nc.scalar.copy(
                out=dst.rearrange("p (g s u) -> p g s u", u=2, s=NP),
                in_=src.rearrange("p (g u s) -> p g s u", u=2, s=NP),
            )

        def quantize(codes, scales, src):
            nc.vector.quantize_mx(out=codes.bitcast(FP8X4), scales=scales, in_=src.bitcast(BF16))

        def sorting_view(ap):
            return ap.rearrange("s (p u e) -> s u p e", u=2, e=2)

        def sorted_view(ap):
            return ap.rearrange("s (u p e) -> s u p e", u=2, e=2)

        def spread(bank, src, first):
            for m in range(4):
                turn(bank, m, src[:, first + m:first + m + 1].to_broadcast([NP, NP]))

        def turn_vectors():
            bank = take_bank()
            turn(bank, 0, rows[:])
            nc.scalar.copy(out=cols[:], in_=banks[bank][:, 0:2 * PANEL_ROW])
            free.append(bank)

        def spread_root():
            bank = take_bank()
            spread(bank, root_cols, 0)
            nc.scalar.copy(
                out=root[:].rearrange("s (g u h b) -> s g u h b", g=2, u=2, b=2),
                in_=banks[bank][:].rearrange("s (b u g h) -> s g u h b", g=2, u=2, b=2),
            )
            free.append(bank)

        def spread_panel(third):
            bank = take_bank()
            spread(bank, cols, PANEL_ROW + 4 * third)
            nc.scalar.copy(out=panel[:, third * BANK:(third + 1) * BANK], in_=banks[bank][:])
            free.append(bank)

        def interleave_inc(h):
            for engine_copy, lo, hi in ((nc.vector.tensor_copy, 0, INC_SPLIT), (nc.scalar.copy, INC_SPLIT, BANK)):
                engine_copy(
                    out=inc_in[h][:, 4 * lo:4 * hi].rearrange("p (c i t) -> p c t i", i=4, t=4),
                    in_=inc_raw[:, :, h * BANK + lo:h * BANK + hi].rearrange("p t (c i) -> p c t i", i=4),
                )

        def quant_inc(h):
            nc.vector.quantize_mx(out=inc_codes[h][:].bitcast(FP8X4), scales=inc_scales[h][:], in_=inc_in[h][:])

        def sort_ref(j):
            nc.scalar.copy(
                out=ref_sorted[j % 2][:].rearrange("s (g u p) -> s g p u", u=2, p=NP),
                in_=ref[j][:].rearrange("s (g p u) -> s g p u", u=2, p=NP),
            )

        def turn_ref(j):
            for half in range(2):
                bank = take_bank()
                for g in range(2):
                    for u in range(2):
                        first = PAIRS * (2 * half + g)
                        if j == 0:
                            words = ref_first[half][:, PAIRS * g + u:PAIRS * (g + 1):2]
                        elif j < FIRST_SORTED:
                            words = ref[j][:, first + u:first + PAIRS:2]
                        else:
                            words = ref_sorted[j % 2][:, first + u * NP:first + (u + 1) * NP]
                        turn(bank, 2 * g + u, words)
                pair_up(ref_in[j % 2][:, half * BANK:(half + 1) * BANK], banks[bank][:])
                free.append(bank)

        def quant_ref(j, lo, hi):
            c = slice(lo * NP, hi * NP)
            quantize(ref_codes[j % 2][:, c], ref_sc[j % 2][:, c], ref_in[j % 2][:, lo * PAIRS:hi * PAIRS])

        def quant_placed(j):
            quantize(pl_codes[j % 2][:], pl_sc[j % 2][:], pl_in[j % 2][:])

        panel_bf = panel[:].bitcast(BF16)
        root_bf = root[:].bitcast(BF16)
        e_banks = {}
        g_banks = {}

        def embed_ref(j, h, passes):
            for g in passes:
                if g == 0:
                    e_banks[(j, h)] = take_bank()
                c = slice(g * NP, (g + 1) * NP)
                nc.tensor.matmul_mx(
                    out=banks[e_banks[(j, h)]][:],
                    lhsT=ref_codes[j % 2][:, c].bitcast(FP8X4), lhsT_scale=ref_sc[j % 2][:, c],
                    rhs=w_codes[g // 2][:, g % 2, 2 * h * BANK:2 * (h + 1) * BANK].bitcast(FP4X4),
                    rhs_scale=w_scales[:, g, h * BANK:(h + 1) * BANK],
                    start=(g == 0), stop=False,
                )

        def embed_placed(j, h):
            nc.tensor.matmul_mx(
                out=banks[e_banks[(j, h)]][:], lhsT=pl_codes[j % 2][:].bitcast(FP8X4), lhsT_scale=pl_sc[j % 2][:],
                rhs=inc_codes[h][:].bitcast(FP8X4), rhs_scale=inc_scales[h][:],
                start=False, stop=True,
            )

        def embed(j, h):
            embed_ref(j, h, range(REF_PASSES))
            embed_placed(j, h)

        def scale_e(j, h):
            nc.vector.tensor_tensor(
                out=sorted_view(e_bf[E_PASSES * (j % 2) + h][:].bitcast(BF16)),
                in0=sorting_view(banks[e_banks[(j, h)]][:]),
                in1=sorted_view(root_bf[:, h * BANK:(h + 1) * BANK]),
                op=MULT,
            )
            free.append(e_banks[(j, h)])

        def turn_e(j):
            bank = take_bank()
            for g in range(E_PASSES):
                for u in range(2):
                    turn(bank, 2 * g + u, e_bf[E_PASSES * (j % 2) + g][:, u * NP:(u + 1) * NP])
            pair_up(e_in[j % 2][:], banks[bank][:])
            free.append(bank)

        def quant_e(j):
            quantize(e_codes[j % 2][:], e_sc[j % 2][:], e_in[j % 2][:])

        def gram(j, groups):
            for n in groups:
                g_banks[(j, n)] = take_bank()
                for g in range(E_PASSES):
                    c = slice(g * NP, (g + 1) * NP)
                    nc.tensor.matmul_mx(
                        out=banks[g_banks[(j, n)]][:],
                        lhsT=e_codes[j % 2][:, c].bitcast(FP8X4), lhsT_scale=e_sc[j % 2][:, c],
                        rhs=r_codes[n][:, g, :].bitcast(FP8X4), rhs_scale=r_scales[:, g, n * BANK:(n + 1) * BANK],
                        start=(g == 0), stop=(g == E_PASSES - 1),
                    )

        def shift(j, n):
            c = slice(n * BANK, (n + 1) * BANK)
            nc.vector.scalar_tensor_tensor(
                out=y[j % 3][:, c], in0=banks[g_banks[(j, n)]][:], scalar=cols[:, j:j + 1], in1=panel_bf[:, c],
                op0=MULT, op1=ADD,
            )
            free.append(g_banks[(j, n)])

        def weigh(engine, j, n, count=1):
            c = slice(n * BANK, (n + count) * BANK)
            engine.tensor_tensor(
                out=y[j % 3][:, c], in0=y[j % 3][:, c], in1=panel_bf[:, P + c.start:P + c.stop], op=MULT,
            )

        def round_y(j, n):
            nc.scalar.copy(
                out=sorted_view(y_bf[Y_GROUPS * (j % 2) + n][:].bitcast(BF16)),
                in_=sorting_view(y[j % 3][:, n * BANK:(n + 1) * BANK]),
            )

        def weigh_rounded(j, n):
            c = slice(n * BANK, (n + 1) * BANK)
            nc.vector.tensor_tensor(
                out=sorted_view(y_bf[Y_GROUPS * (j % 2) + n][:].bitcast(BF16)), in0=sorting_view(y[j % 3][:, c]),
                in1=sorting_view(panel_bf[:, P + c.start:P + c.stop]), op=MULT,
            )

        def store_y(j, n, count=1):
            c = slice(n * BANK, (n + count) * BANK)
            nc.sync.dma_start(out=out_0[j * NP:(j + 1) * NP, c], in_=y[j % 3][:, c])

        def y_words(j, n):
            src = y_bf[Y_GROUPS * (j % 2) + n]
            return [src[:, u * NP:(u + 1) * NP] for u in range(2)]

        def y_in(j, n):
            return y_in01[j % 3][:, n * PAIRS:(n + 1) * PAIRS] if n < 2 else y_in2[j % 3][:]

        def turn_y01(j):
            bank = take_bank()
            for n in range(2):
                for u in range(2):
                    turn(bank, 2 * n + u, y_words(j, n)[u])
            pair_up(y_in01[j % 3][:], banks[bank][:])
            free.append(bank)

        def turn_halves(y_groups, placed_tiles):
            bank = take_bank()
            halves = [(y_in(j, n), y_words(j, n)) for j, n in y_groups]
            for j in placed_tiles:
                halves.append((pl_in[j % 2][:], [placed[j][:, u:PAIRS:2] for u in range(2)]))
            for k, (dst, words) in enumerate(halves):
                for u in range(2):
                    turn(bank, 2 * k + u, words[u])
            for k, (dst, words) in enumerate(halves):
                pair_up(dst, banks[bank][:, k * PAIRS:(k + 1) * PAIRS])
            free.append(bank)

        def quant_y(j, groups):
            run, lo, hi = run_of(CODE_RUNS, j)
            sc_run, sc_lo, sc_hi = run_of(SCALE_RUNS, j)
            for n in groups:
                quantize(
                    y_codes[run][:, n, (j - lo) * NP:(j - lo + 1) * NP],
                    y_sc[sc_run][:, n, (j - sc_lo) * NP:(j - sc_lo + 1) * NP], y_in(j, n),
                )
            if j == hi - 1:
                dst = out_1.rearrange("g p m t -> p g (m t)").bitcast(I32)[:, :, lo * NP:hi * NP]
                nc.sync.dma_start(out=dst, in_=y_codes[run][:].bitcast(I32))
            if j == sc_hi - 1:
                for q in range(4):
                    queue = nc.scalar if j == LAST and q % 2 == 1 else nc.sync
                    dst = out_2.bitcast(I32)[:, 4 * q:4 * q + 4, sc_lo * NP // 4:sc_hi * NP // 4]
                    queue.dma_start(
                        out=dst.rearrange("g r w -> r g w"), in_=y_sc[sc_run][32 * q:32 * q + 4, :, :].bitcast(I32),
                    )

        def shift_all(j):
            shift(j, 0)
            weigh(nc.gpsimd, j, 0)
            shift(j, 1)
            shift(j, 2)

        def weigh_rest(j):
            weigh(nc.vector, j, 1, Y_GROUPS - 1)
            store_y(j, 0, Y_GROUPS)

        turn_ref(0)
        spread_root()
        quant_ref(0, 0, 2)
        quant_ref(0, 2, 4)
        nc.vector.tensor_copy(out=rows[0:PANEL_ROW, :], in_=sw_rows[:])
        for h in range(E_PASSES):
            embed_ref(0, h, [0, 1])
        turn_ref(1)
        quant_ref(1, 0, 2)
        quant_ref(1, 2, 4)
        for h in range(E_PASSES):
            embed_ref(0, h, [2, 3])
        for h in range(E_PASSES):
            interleave_inc(h)
        turn_halves([], [0, 1])
        turn_vectors()
        quant_inc(0)
        quant_placed(0)
        quant_inc(1)
        quant_placed(1)
        for h in range(E_PASSES):
            embed_ref(1, h, range(REF_PASSES))
        turn_ref(2)
        turn_halves([], [2])
        for j in range(2):
            for h in range(E_PASSES):
                embed_placed(j, h)
        scale_e(0, 0)
        scale_e(0, 1)
        quant_ref(2, 0, REF_PASSES)
        quant_placed(2)
        spread_panel(0)
        turn_e(0)
        spread_panel(1)
        spread_panel(2)
        scale_e(1, 0)
        quant_e(0)
        scale_e(1, 1)
        embed(2, 0)
        gram(0, ALL_GROUPS)
        sort_ref(3)
        scale_e(2, 0)
        turn_e(1)
        shift_all(0)
        quant_e(1)
        weigh_rest(0)
        turn_ref(3)
        turn_halves([], [3])
        for n in ALL_GROUPS:
            round_y(0, n)
        sort_ref(4)
        quant_placed(3)
        quant_ref(3, 0, REF_PASSES)
        embed(2, 1)
        scale_e(2, 1)
        gram(1, ALL_GROUPS)

        for j in range(3, TILES):
            j_in, j_e, j_g, j_y = j + 1, j - 1, j - 2, j - 3
            turn_e(j_e)
            turn_y01(j_y)
            turn_halves([(j_y, 2)], [j_in] if live(j_in) else [])
            shift_all(j_g)
            weigh_rest(j_g)
            if live(j_in):
                turn_ref(j_in)
            for n in ALL_GROUPS:
                round_y(j_g, n)
            if live(j_in + 1):
                sort_ref(j_in + 1)
            quant_e(j_e)
            quant_y(j_y, ALL_GROUPS)
            embed(j, 0)
            scale_e(j, 0)
            if live(j_in):
                quant_placed(j_in)
                quant_ref(j_in, 0, REF_PASSES)
            embed(j, 1)
            scale_e(j, 1)
            if j < LAST:
                gram(j_e, ALL_GROUPS)

        prev = LAST - 1
        gram(prev, [0, 1])
        turn_e(LAST)
        turn_y01(prev - 1)
        turn_halves([(prev - 1, 2)], [])
        gram(prev, [2])
        shift(prev, 0)
        shift(prev, 1)
        weigh(nc.vector, prev, 0)
        quant_e(LAST)
        gram(LAST, ALL_GROUPS)
        store_y(prev, 0)
        quant_y(prev - 1, ALL_GROUPS)
        round_y(prev, 0)
        shift(prev, 2)
        weigh(nc.vector, prev, 1)
        store_y(prev, 1)
        round_y(prev, 1)
        weigh(nc.gpsimd, prev, 2)
        store_y(prev, 2)
        turn_y01(prev)
        round_y(prev, 2)
        for n in ALL_GROUPS:
            shift(LAST, n)
        for n in range(2):
            weigh(nc.vector, LAST, n)
            round_y(LAST, n)
            store_y(LAST, n)
        weigh_rounded(LAST, 2)
        weigh(nc.vector, LAST, 2)
        store_y(LAST, 2)
        turn_halves([(prev, 2)], [])
        ready_order = [0, 2, 1]
        for n in ready_order:
            turn_halves([(LAST, n)], [])
        quant_y(prev, ALL_GROUPS)
        quant_y(LAST, ready_order)
